import numpy as np, ml_dtypes
CORES = [5,29,101,125,133,157,229,253]
N = 8
BF = ml_dtypes.bfloat16
def gentries(a):
    return np.ascontiguousarray(a.reshape(8, 16, -1).transpose(0, 2, 1)).reshape(8, -1)
def gtable(e):
    e = np.asarray(e); return np.ascontiguousarray(e.reshape(8, -1, 16).transpose(0, 2, 1)).reshape(128, -1).astype(np.int32)
S, LEN, RO = 448, 20, 4
W = N * S
FARTHEST = 2 ** 23
def parts(rng):
    own = S * np.arange(N)[:, None, None, None] + np.arange(S)[None, None, :, None]
    sc = np.exp2(3 + (np.log2(W) - 3.5) * rng.random((N, 8, 1, 16)))
    rf = (own + np.rint(sc * rng.standard_normal((N, 8, S, 16))).astype(np.int64)) % W
    hi = rng.integers(40, 256, (N, 8, 16, 1)); sz = 16 + (rng.random((N, 8, 16, S)) * (hi - 15)).astype(np.int64)
    lim = 135 * sc * np.where(sc > S // 2, 8, 1) * np.exp2(2 * rng.random((N, 8, 1, 16))) * (0.8 + 0.4 * rng.random((N, 8, 16, 16)))
    return np.minimum(sz, 255), rf, np.minimum(lim.astype(np.int64), FARTHEST)
def kinds(rng, fold, decoy, chain, strange):
    u = rng.random((N, 8, S)); k = np.where(u < fold, rng.integers(1, RO + 1, u.shape), 0); lo = fold
    for share, c in ((decoy, RO + 1), (chain, RO + 2), (strange, RO + 3)):
        k = np.where((u >= lo) & (u < lo + share), c, k); lo = lo + share
    k[..., S - RO:] = np.argsort(rng.random((N, 8, RO)), axis=-1) + 1; k[..., 0] = 0
    return k
def weave(rng, rf, kind, first=False):
    n = np.arange(S)
    def earlier(ok):
        order = np.argsort(~ok, axis=-1, kind="stable"); cnt = np.add.accumulate(ok.astype(np.int64), axis=-1) - ok
        j = np.minimum((rng.random(ok.shape) * cnt).astype(np.int64), np.maximum(cnt - 1, 0))
        return np.where(cnt > 0, np.take_along_axis(order, j, -1), n)
    def of(a, i): return np.take_along_axis(a, i[..., None], 2)
    rf = rf.copy(); m = (kind >= 1) & (kind <= RO); dec = kind == RO + 1
    root = np.zeros(kind.shape, np.int64) if first else earlier(kind == 0)
    cd = np.where(m | dec | (kind == RO + 3), root, n)
    cdw = (cd + S * np.arange(N)[:, None, None]).transpose(1, 0, 2).reshape(8, W)
    pos = np.ascontiguousarray(np.argsort(rng.random((N, 8, S, 16)), axis=-1)[..., :RO - 1]); x = np.zeros((N, 8, S, RO - 1), np.int64)
    for g in range(8):
        flat = kind[:, g].reshape(-1)
        for l in range(1, RO): x[:, g, :, l - 1] = rng.choice(np.flatnonzero(flat == l), (N, S))
    y = cdw[np.arange(8)[None, :, None, None], x]
    flip = rng.random(x.shape) < 0.4; x, y = np.where(flip, y, x), np.where(flip, x, y)
    np.put_along_axis(rf, pos, np.where((kind == 0)[..., None], y, np.take_along_axis(rf, pos, -1)), -1)
    base, bp, bx = of(rf, cd), of(pos, cd), of(x, cd)
    for l in range(1, RO):
        use = m & ((kind == l + 1) | ((kind > l + 1) & (rng.random(kind.shape) < 0.5))); p = bp[..., l - 1:l]
        np.put_along_axis(base, p, np.where(use[..., None], bx[..., l - 1:l], np.take_along_axis(base, p, -1)), -1)
    p = bp[..., :1]; v = np.take_along_axis(base, p, -1)
    np.put_along_axis(base, p, np.where(dec[..., None], (v // S + 1) % N * S, v), -1)
    rf = np.where((m | dec)[..., None], base, rf)
    c2 = earlier(m); ch = (kind == RO + 2) & (c2 != n)
    cd = np.where(ch, c2, cd); rl = of(rf, cd); pl = of(bp, cd)[..., :1]
    late = ch & (np.take_along_axis(kind, cd, -1) == 1) & (rng.random(kind.shape) < 0.6)
    np.put_along_axis(rl, pl, np.where(late[..., None], of(bx, cd)[..., :1], np.take_along_axis(rl, pl, -1)), -1)
    return np.where(ch[..., None], rl, rf), cd
def pack(sz, rf, cd, rch):
    return {"sz": np.ascontiguousarray(sz.reshape(N, 128, S)).astype(np.int32), "rf": np.ascontiguousarray(rf.transpose(0, 1, 3, 2)).reshape(N, 128, S).astype(np.int32),
            "cd": np.stack([gtable(a) for a in cd]), "rch": np.ascontiguousarray(rch.reshape(N, 128, 16)).astype(np.int32)}
def half():
    return (np.arange(N)[:, None] + np.arange(8)[None, :]) % 2 == 0
def setup_inputs(rng):
    sz, rf, rch = parts(rng); rf, cd = weave(rng, rf, kinds(rng, 0.24, 0.06, 0.06, 0.04))
    return pack(sz, rf, cd, rch)
def setup_inputs_spread(rng):
    sz, rf, rch = parts(rng)
    sz = 16 + (240 * np.power(rng.random((N, 8, 16, S)), np.exp2(rng.integers(-2, 4, (N, 8, 1, S))))).astype(np.int64)
    rch = np.exp2(4 + 18 * rng.random((N, 8, 1, 16)) + 3 * rng.random((N, 8, 16, 16))).astype(np.int64)
    rf, cd = weave(rng, rf, kinds(rng, 0.2, 0.08, 0.08, 0.08))
    return pack(np.minimum(sz, 255), rf, cd, np.minimum(rch, FARTHEST))
def setup_inputs_ends(rng):
    sz = np.where(rng.random((N, 8, 16, S)) < 0.5, 16, 255); sz[:, :, [1, 15]] = 255; sz[:, :, [0, 14]] = 16
    k = kinds(rng, 0.05, 0.08, 0.0, 0.55); k[:, 1::2, S - 1] = 0
    for g in range(0, 8, 2): k[N - 1, g, S - 1] = 1 + (g >> 1) % (RO - 1)
    m = 2 ** 20 // (S * (252 + 9 * LEN))
    many = (2 ** 20 / (S * m * (1 - np.mean(k == 1))) - 255) / LEN
    few = np.floor(many * np.arange(8 * N + 1)).astype(np.int64); few = 16 - (few[1:] - few[:-1]).reshape(N, 8, 1, 1)
    o = rng.random((N, 8, 1, 16)); o[..., 0] = -1; o[..., 15] = 2; o[:N - m, ::2, :, 15] = -1
    late = np.argsort(np.argsort(o, axis=-1), axis=-1) < few
    zero = rng.random((N, 8, 16, 16)) < 0.5; zero[:, :, np.arange(16), np.arange(16)] = True
    rch = np.where(late | ~zero, FARTHEST, 0)
    away = np.where(2 * np.arange(N) < N, W - 1, 0)[:, None, None, None]
    rf = np.where(rng.random((N, 8, S, 16)) < 0.5, 0, W - 1); rf = np.where(late & (rng.random(rf.shape) < 0.8), away, rf)
    rf, cd = weave(rng, rf, k, True)
    n = np.arange(S); own = S * np.arange(N)[:, None, None] + n
    fold = (cd != n) & np.all(rf == np.take_along_axis(rf, cd[..., None], 2), axis=-1)
    cnt = np.add.reduce(((rf != own[..., None]) & ~late).astype(np.int64), axis=-1)
    ln = np.where(fold, 0, 255 + LEN * cnt).reshape(-1); at = np.add.accumulate(ln) - ln
    gone = fold.reshape(-1).copy(); free = (((k == 0) | (k > RO)) & ~fold).reshape(-1); less = 0; last = 0
    for q in range(N - m):
        for g in range(8):
            ks = np.flatnonzero(late[q, g, 0]); ws = rng.permutation(1 + np.flatnonzero(k[q, g, 1:S // 4] == RO + 3))
            for i in range(2):
                vs = rng.permutation(np.arange((1 + i) * S // 4, (2 + i) * S // 4 - 12)); vs = vs[k[q, g, vs] == RO + 3]
                if i == 0: vs = vs[at[(q * 8 + g) * S + vs] % 2 == 1]
                if len(vs) == 0 or len(ws) < 2: continue
                v, w = int(vs[0]), int(ws[i])
                want = int(at[(q * 8 + g) * S + v]) + FARTHEST + i * int(rng.integers(0, 2)) + less
                u = int(np.searchsorted(at, want)); b = u % S
                if u // S != (q + m) * 8 + g or b < 8 or b >= S - 8 or u - 8 < last: continue
                cuts = [j for j in range(u - 1, u - 7, -1) if not gone[j]][:3]
                if len(cuts) < 3 or not (free[u] and free[u + 1]): continue
                rest = int(at[u]) - want; less += rest
                for j in cuts:
                    cut = min(rest, 239); rest -= cut
                    sz[j // (8 * S), j // S % 8, [1, 15], j % S] -= cut
                to = (q + m) * S + b
                if i == 0:
                    cd[q + m, g, b] = 0; cd[q + m, g, b + 1] = b; rf[q + m, g, [b, b + 1]] = rf[q + m, g, 0]
                    gone[u] = True; gone[u + 1] = True; less += int(ln[u] + ln[u + 1]); to += 1
                last = u + 1
                kk = int(ks[-1]) if i == 0 else int(rng.choice(ks)); p = int(rng.choice(np.flatnonzero(~late[q, g, 0])))
                x = int(rng.choice(np.flatnonzero(fold[:, g].reshape(-1)))); y = x // S * S + int(cd[x // S, g, x % S])
                rf[q, g, w] = rf[q, g, v]; rf[q, g, [w, v], kk] = to
                rf[q, g, w, p], rf[q, g, v, p] = (y, x) if rng.random() < 0.5 else (x, y)
                cd[q, g, v] = w
    return pack(sz, rf, cd, rch)
def setup_inputs_corners(rng):
    sz, rf, rch = parts(rng); k = kinds(rng, 0.24, 0.06, 0.1, 0.04); other = half(); k[other] = RO + 4
    rf, cd = weave(rng, rf, k); n = np.arange(S)
    for q, g in np.argwhere(other).tolist():
        t = (g // 2 + q) % 6; o = q * S; few = np.array([0, W - 1, o, o + S - 1, o + S // 2, (q + 1) % N * S + S - 1])
        if t < 3:
            rf[q, g] = rng.permutation(np.concatenate([few, rng.choice(few, 10)])); cd[q, g] = (np.maximum(n - 1, 0), 0 * n, n)[t]
        elif t == 3:
            rf[q, g] = (o + n)[:, None]; cd[q, g] = np.maximum(n - 1, 0)
        elif t == 4:
            cd[q, g] = np.minimum((rng.random(S) * (n + 1)).astype(np.int64), n); rch[q, g] = FARTHEST; sz[q, g] = 255
        else:
            j = rng.integers(0, 3, (S, 16)); rf[q, g] = np.where(j == 0, 0, np.where(j == 1, W - 1, (o + n)[:, None]))
            cd[q, g] = np.where(n % 2 == 1, 0, n); sz[q, g] = rng.choice(np.array([16, 255]), (16, S))
        if t in (2, 3, 5): rch[q, g] = 0
    return pack(sz, rf, cd, rch)
def setup_inputs_crowd(rng):
    sz, rf, rch = parts(rng); k = kinds(rng, 0.24, 0.06, 0.06, 0.04); other = half(); k[other] = RO + 4
    rf, cd = weave(rng, rf, k); n = np.arange(S)
    for q, g in np.argwhere(other).tolist():
        t = (g // 2 + q) % 4; pool = np.flatnonzero(k[:, g].reshape(-1) == 1 + (g // 2) % (RO - 1))
        rf[q, g] = int(rng.choice(pool)); rch[q, g] = 0; sz[q, g, ::2] = 255; sz[q, g, 1::4] = 16
        if t == 1: rf[q, g, :, int(rng.integers(0, 16))] = q * S + n
        if t == 2: cd[q, g] = np.minimum((rng.random(S) * n).astype(np.int64), np.maximum(n - 1, 0))
        if t == 3:
            rf[q, g] = rng.choice(pool, 4)[rng.integers(0, 4, 16)]; rf[q, g, S - 1, 15] = q * S + S - 1; cd[q, g] = 0
    return pack(sz, rf, cd, rch)
def setup_inputs_calm(rng):
    sz, rf, rch = parts(rng); k = kinds(rng, 0.24, 0.06, 0.06, 0.04); other = half(); k[other] = RO + 4
    rf, cd = weave(rng, rf, k); n = np.arange(S); m = S // 4 - 1
    for q, g in np.argwhere(other).tolist():
        o = q * S; dist = int(rng.integers(370, 401)); i = int(rng.integers(0, 16)); big = rng.random(m) < 0.4
        b = np.where(big, rng.integers(15, 17, m), rng.integers(0, 4, m)); c = np.where(big, rng.integers(15, 17, m), rng.integers(1, 4, m))
        e = (rng.random((3, m)) < np.array([[0.8], [0.75], [0.5]])).astype(np.int64)
        s1 = np.where(big, rng.integers(17, 35, m), rng.integers(150, 181, m))
        s0 = dist - LEN * b + e[0] - s1; s2 = dist - LEN * c + e[1] - s1; s3 = dist - LEN * c + e[2] - s2
        sz[q, g, i, :4 * m] = np.stack([s3, s2, s1, s0], axis=1).reshape(-1)
        rch[q, g] = FARTHEST; rch[q, g, i] = dist
        put = np.argsort(rng.random((m, 4, 16)), axis=-1) < np.stack([c, c, c, b], axis=1)[..., None]
        self_ = np.repeat((o + n)[:, None], 16, axis=1); to = self_[:4 * m].reshape(m, 4, 16) + 2
        to[:, 3] = (q + rng.integers(1, N, (m, 16))) % N * S + rng.integers(0, S, (m, 16))
        self_[:4 * m] = np.where(put, to, to * 0 + self_[:4 * m].reshape(m, 4, 16)).reshape(4 * m, 16)
        rf[q, g] = self_; cd[q, g] = np.minimum((rng.random(S) * (n + 1)).astype(np.int64), n)
    return pack(sz, rf, cd, rch)
def check_inputs(d):
    bad = []
    for k, lo, hi in (("sz", 16, 255), ("rf", 0, W - 1), ("cd", 0, S - 1), ("rch", 0, FARTHEST)):
        if np.min(d[k]) < lo or np.max(d[k]) > hi: bad.append("range of " + k)
    if any(np.any(gentries(a) > np.arange(S)) for a in d["cd"]): bad.append("cd names a later section")
    return bad
def places(z):
    t = np.ascontiguousarray(z.transpose(2, 0, 1, 3)).reshape(16, N * 8 * S)
    return np.ascontiguousarray((np.add.accumulate(t, axis=1) - t).reshape(16, N, 8, S).transpose(1, 2, 0, 3))
def reference(sz, rf, cd, rch):
    z = sz.astype(np.int64).reshape(N, 8, 16, S); lim = rch.astype(np.int64).reshape(N, 8, 16, 16)
    r = np.stack([gentries(a) for a in rf]).astype(np.int64).reshape(N, 8, S, 16); c = np.stack([gentries(a) for a in cd]).astype(np.int64)
    first = S * np.arange(N)[:, None, None]; n = np.arange(S)
    far = np.zeros((N, 8, S, 16), bool); gone = np.zeros((N, 8, S), bool); j = np.zeros((N, 8, S), np.int64) + first + n
    for rnd in range(RO):
        jw = j.transpose(1, 0, 2).reshape(8, W)
        r = jw[np.arange(8)[None, :, None, None], r]
        a = places(z); aw = np.ascontiguousarray(a.transpose(1, 2, 0, 3)).reshape(8, 16, W)
        now = np.zeros((N, 8, S, 16), bool)
        for q in range(N):
            for g in range(8):
                d = np.abs(aw[g][:, r[q, g]] - a[q, g][:, :, None])
                now[q, g] = np.any(d > lim[q, g][:, None, :], axis=0)
        new = now & ~far & ~gone[..., None]; far = far | new
        like = np.all(r == np.take_along_axis(r, c[..., None], 2), axis=-1)
        fold = ~gone & (c != n) & like
        grow = LEN * np.add.reduce(new.astype(np.int64), axis=-1)
        z = np.where(fold[:, :, None, :], 0, z + grow[:, :, None, :])
        gone = gone | fold; j = np.where(gone, first + c, first + n)
    return {"yr": np.ascontiguousarray(r.transpose(0, 1, 3, 2)).reshape(N, 128, S).astype(np.float32), "yj": j.astype(np.float32),
            "yf": np.ascontiguousarray(far.transpose(0, 1, 3, 2)).reshape(N, 128, S).astype(np.float32), "ya": places(z).reshape(N, 128, S).astype(np.float32)}

@@ -1,0 +1,589 @@
+from concourse.bass import DstId, RemoteDMATransfer
+from concourse.mybir import AluOpType as A, ActivationFunctionType as F
+
+N, S, RO = 8, 448, 4
+W = N * S
+CEN = 131072.0
+K = 8781824.0
+CPOS = 0.5 * K + CEN
+CNEG = 1.5 * K + 1 + CEN
+MID = 13800000.0
+BIG = 67108864.0
+CH = 7
+
+SB = lambda n, d="float32": ("sbuf", [128, n], d)
+SCRATCH = {
+    "s1": ("dram", [N, 128, 64], "int32"), "r1": ("dram", [N, 128, 64], "int32"),
+    "s2": ("dram", [N, 128, 112], "uint16"), "r2": ("dram", [N, 128, 112], "uint16"),
+    "s3": ("dram", [N, 128, 64], "float32"), "r3": ("dram", [N, 128, 64], "float32"),
+    "s4": ("dram", [N, 128, 56], "bfloat16"), "r4": ("dram", [N, 128, 56], "bfloat16"),
+    "xs": SB(5 * 64), "xr": SB(5 * 64),
+    "pi": SB(8, "int32"), "pf": SB(16), "ion": SB(S), "nc": SB(S), "ncb": SB(S, "bfloat16"), "i38": SB(128, "bfloat16"), "i35": SB(128, "bfloat16"), "zr": SB(128, "bfloat16"), "ez": SB(256), "thr": SB(S), "ones": SB(S),
+    "onesb": SB(S, "bfloat16"), "kv": SB(128, "bfloat16"), "cm": SB(128), "cdv": SB(128), "rv": SB(64), "gv": SB(64),
+    "mw": SB(64), "mo": SB(64), "mf": SB(64), "t64": SB(64), "u64": SB(64),
+    "shw": SB(256, "bfloat16"), "i1k": SB(128, "bfloat16"), "ibig": SB(128, "bfloat16"), "i16": SB(128, "bfloat16"),
+    "i32": SB(128, "bfloat16"), "idf": SB(128), "swp": SB(128), "ww": SB(144, "bfloat16"), "uw": SB(144, "bfloat16"),
+    "b20": SB(128, "bfloat16"), "b512": SB(128, "bfloat16"), "em": SB(128), "lm": SB(128), "rep": SB(128, "bfloat16"),
+    "ct": SB(8), "sg": SB(16), "cv": SB(16), "t16": SB(16), "u16": SB(16), "rot": SB(2, "uint16"),
+    "ja": SB(28), "jb": SB(28), "jc": SB(28), "ji": SB(28, "int32"), "jk": SB(28, "int32"), "pl": SB(28, "uint16"),
+    "szo": SB(S, "int32"), "rfo": SB(S, "int32"), "szob": SB(S, "bfloat16"), "yo": SB(S), "to": SB(S), "lo": SB(S),
+    "yw": SB(2 * S), "m2": SB(2 * S, "uint16"), "jrow": SB(S), "al8": SB(S, "bfloat16"), "faro": SB(S, "bfloat16"),
+    "yff": SB(S), "yaf": SB(S),
+    "szi": SB(S, "int32"), "cdi": SB(28, "int32"), "rci": SB(16, "int32"), "szb": SB(S, "bfloat16"),
+    "cdl": SB(28, "uint16"), "bk": SB(16), "cb": SB(S, "bfloat16"), "lt": SB(S, "uint16"), "ynu": SB(S, "uint16"),
+    "ln": SB(S), "tot": SB(8), "loc": SB(S), "hi": SB(S, "bfloat16"), "lw": SB(S, "bfloat16"),
+    "tab": SB(9 * S), "jt": SB(9 * S, "bfloat16"), "gr": SB(16 * S, "bfloat16"), "gg": SB(16 * S),
+    "ind": SB(16 * S, "bfloat16"), "bs": SB(8), "ro": SB(16), "c1": SB(16), "cs": SB(16),
+    "ta": SB(S, "bfloat16"), "tb": SB(S, "bfloat16"), "tc": SB(S),
+    "ref": SB(S), "neg": SB(S, "bfloat16"), "mis": SB(S, "bfloat16"), "al": SB(2 * S, "bfloat16"), "jv": SB(S, "bfloat16"),
+    "nth": SB(S), "far": SB(2 * S, "bfloat16"), "yrf": SB(S), "yjf": SB(S),
+}
+for _b in range(8):
+    SCRATCH["p%d" % _b] = ("psum", [128, 512], "float32")
+SEMAPHORES = (["cV", "cS", "cP", "cG", "out", "m1", "m2", "m3", "m4", "dg"] + ["xr%d" % t for t in range(5)]
+              + ["dsz", "drf", "ds1", "dr1", "dw1", "dw1b", "ds2", "dw2", "dw2b", "dj0", "dj1", "dj2", "ds3", "do3", "dy", "ds4", "do4"])
+
+
+def plan(T, topo, r):
+    me = T.cores[r]
+    others = [d for d in range(N) if d != r]
+    direct = [d for d in others if topo.may_write(me, T.cores[d])]
+    away = [d for d in others if d not in direct]
+    able = [c for c in topo.cores_of(me) if c != me and all(topo.may_write(c, T.cores[d]) for d in away)]
+    bulk = {d: able[i % len(able)] for i, d in enumerate(away)}
+    per = N // len(able)
+    small = [(c, (away + direct)[i * per:(i + 1) * per]) for i, c in enumerate(able)]
+    return direct, away, bulk, small
+
+
+def bits(engs):
+    m = 0
+    for e in engs:
+        m |= 1 << e
+    return m
+
+
+def share(engs, parts):
+    n = 1
+    while 2 * n * parts <= len(engs):
+        n *= 2
+    return [engs[i * n:(i + 1) * n] for i in range(parts)]
+
+
+def xfer(topo, src, dst, a, b, engs, sem):
+    rid, pid = topo.addr(dst, src)
+    return RemoteDMATransfer(dst_ids=[DstId(rid=rid, pnc=pid)], dma_engine_mask=bits(engs), remote_sem=sem, src=a, dst=b)
+
+
+def split(T, topo, r):
+    me = T.cores[r]
+    direct, away, bulk, small = plan(T, topo, r)
+    off = topo.engines(me, T.cores[direct[0]])
+    on = [e for e in topo.engines(me, small[0][0]) if e not in off]
+    return off, on
+
+
+ORDER = ["m1", "x0", "m2", "x1", "x2", "x3", "m3", "x4", "m4"]
+
+
+def helper(g, core, T, topo):
+    rs = [r for r in range(N) if core in topo.cores_of(T.cores[r])]
+    if not rs:
+        return
+    r = rs[0]
+    direct, away, bulk, small = plan(T, topo, r)
+    off, on = split(T, topo, r)
+    mine = [d for d in away if bulk[d] == core]
+    few = [ds for c, ds in small if c == core]
+    sent = 0
+    for m in ORDER:
+        if m[0] == "m" and mine:
+            buf = T["r" + m[1]]
+            g.wait_ge(T.sem[m], len(share(on, len(away))[0]) * len(mine))
+            es = share(topo.engines(core, T.cores[mine[0]]), len(mine))
+            g.remote_dma_fused([xfer(topo, core, T.cores[d], buf[d], buf[r], e, T.sem[m]) for d, e in zip(mine, es)], local_sem=T.sem.out)
+            sent += sum(len(e) for e in es)
+        if m[0] == "x" and few:
+            t = int(m[1]); ds = few[0]
+            g.wait_ge(T.sem["xr%d" % t], len(share(on + off, len(small))[0]))
+            es = share(topo.engines(core, T.cores[ds[0]]), len(ds))
+            g.remote_dma_fused([xfer(topo, core, T.cores[d], T.xs[:, 64 * t + 8 * i:64 * t + 8 * i + 8],
+                                     T.xr[:, 64 * t + 8 * r:64 * t + 8 * r + 8], e, T.sem["xr%d" % t])
+                                for i, (d, e) in enumerate(zip(ds, es))], local_sem=T.sem.out)
+            sent += sum(len(e) for e in es)
+    if sent:
+        g.wait_ge(T.sem.out, sent)
+
+
+def rank_program(g, core, T, topo):
+    me = T.rank_of(core)
+    if me is None:
+        return helper(g, core, T, topo)
+    direct, away, bulk, small = plan(T, topo, me)
+    off, on = split(T, topo, me)
+    order = away + direct + [me]
+    Q = {"V": g.vector, "S": g.scalar, "P": g.tensor, "G": g, "Y": g.sync}
+    cnt, seen, wr, rd = {}, {}, {}, {}
+
+    def need(e, tok):
+        s, v = tok
+        if v is None:
+            v = cnt[s]
+        assert v <= cnt[s], (e, tok)
+        if seen.get((e, s), 0) < v:
+            Q[e].wait_ge(T.sem[s], v)
+            seen[(e, s)] = v
+
+    def deps(e, reads, writes):
+        for k in reads:
+            for t in wr.get(k, []):
+                need(e, t)
+            if k[0] == "p" and k[1:].isdigit():
+                for o, t in rd.get(k, {}).items():
+                    if o != e:
+                        need(e, t)
+        for k in writes:
+            for t in wr.get(k, []):
+                if not (e == "P" and t[0] == "cP"):
+                    need(e, t)
+            for o, t in rd.get(k, {}).items():
+                need(e, t)
+
+    def note(e, tok, reads, writes, add=False):
+        for k in reads:
+            rd.setdefault(k, {})[e if tok[0][0] == "c" else tok[0]] = tok
+        for k in writes:
+            wr[k] = (wr.get(k, []) if add else []) + [tok]
+            if not add:
+                rd[k] = {}
+
+    def op(e, fn, reads, writes, inc=True):
+        deps(e, reads, writes)
+        ins = fn()
+        s = "c" + e
+        if inc:
+            cnt[s] = cnt.get(s, 0) + 1
+            ins.then_inc(T.sem[s], 1)
+            note(e, (s, cnt[s]), reads, writes)
+        else:
+            note(e, (s, cnt.get(s, 0) + 1), reads, writes)
+
+    def dma(e, sem, out, in_, reads, writes):
+        fresh = [k for k in writes if (sem, None) not in wr.get(k, [])]
+        deps(e, reads, fresh)
+        Q[e].dma_start(out, in_).then_inc(T.sem[sem], 16)
+        cnt[sem] = cnt.get(sem, 0) + 16
+        note(e, (sem, None), reads, fresh)
+
+    def arrive(sem, n, key, add=False):
+        cnt[sem] = n
+        note("G", (sem, n), [], [key], add)
+
+    def fused(xs, reads, n):
+        deps("G", reads, [])
+        g.remote_dma_fused(xs, local_sem=T.sem.out)
+        cnt["out"] = cnt.get("out", 0) + n
+
+    def bulk_send(i):
+        s, r, sem = T["s%d" % i], T["r%d" % i], "m%d" % i
+        ea, eb = share(off, len(direct)), share(on, len(away))
+        xs = [xfer(topo, core, bulk[d], s[d], r[d], e, T.sem[sem]) for d, e in zip(away, eb)]
+        xs += [xfer(topo, core, T.cores[d], s[d], r[me], e, T.sem[sem]) for d, e in zip(direct, ea)]
+        fused(xs, ["s%d" % i], sum(len(e) for e in ea + eb))
+        n = 0
+        for q in range(N):
+            if q != me:
+                dq, aq, bq, sq = plan(T, topo, q)
+                if me in dq:
+                    n += len(share(split(T, topo, q)[0], len(dq))[0])
+                else:
+                    n += len(share(topo.engines(bq[me], core), sum(1 for d in aq if bq[d] == bq[me]))[0])
+        arrive(sem, n, "r%d" % i, True)
+
+    def sums_send(t, mask, mk):
+        op("S", lambda: g.scalar.activation(T.xs[:, 64 * t:64 * t + 64], mask[:], F.Identity, scale=T.tot[:, t:t + 1]), [mk, "tot%d" % t], ["xs%d" % t])
+        if t < RO:
+            act(T.xr[:, 64 * t + 8 * me:64 * t + 8 * me + 8], mask[:, 56:64], F.Identity, [mk, "tot%d" % t], ["xo%d" % t], scale=T.tot[:, t:t + 1])
+        eb = share(on + off, len(small))
+        wide = 64 // len(small)
+        xs = []
+        for (c, ds), e in zip(small, eb):
+            o = 64 * t + 8 * order.index(ds[0])
+            xs.append(xfer(topo, core, c, T.xs[:, o:o + wide], T.xs[:, 64 * t:64 * t + wide], e, T.sem["xr%d" % t]))
+        fused(xs, ["xs%d" % t], sum(len(e) for e in eb))
+        nr = 0
+        for q in range(N):
+            if q != me:
+                c, ds = [x for x in plan(T, topo, q)[3] if me in x[1]][0]
+                nr += len(share(topo.engines(c, core), len(ds))[0])
+        arrive("xr%d" % t, nr, "xr%d" % t)
+
+    V, Sc, P = g.vector, g.scalar, g.tensor
+
+    def ts(out, in0, s1, s2, o0, o1, reads, writes):
+        if o1 is None:
+            op("V", lambda: V.tensor_scalar(out, in0, s1, None, o0), reads, writes)
+        else:
+            op("V", lambda: V.tensor_scalar(out, in0, s1, s2, o0, o1), reads, writes)
+
+    def tt(out, a, b, o, reads, writes):
+        op("V", lambda: V.tensor_tensor(out, a, b, o), reads, writes)
+
+    def cp(out, a, reads, writes):
+        op("V", lambda: V.tensor_copy(out, a), reads, writes)
+
+    def ms(out, v, writes):
+        op("V", lambda: V.memset(out, v), [], writes)
+
+    def act(out, a, f, reads, writes, **kw):
+        op("S", lambda: Sc.activation(out, a, f, **kw), reads, writes)
+
+    def mm(out, l, r, st, sp, reads, bank, inc=None):
+        op("P", lambda: P.matmul(out, l, r, st, sp), reads, [bank], sp if inc is None else inc)
+
+    def iota(out, pat, base, chm, key, flt=True):
+        if flt:
+            op("G", lambda: g.iota(out, pat, base, chm, allow_small_or_imprecise_dtypes=True), [], [key])
+        else:
+            op("G", lambda: g.iota(out, pat, base, chm), [], [key])
+
+    PB = [T["p%d" % b] for b in range(8)]
+    mine = slice(16 * me, 16 * me + 16)
+    pp, pm, pd = T.pf[:, 0:1], T.pf[:, 1:2], T.pf[:, 2:3]
+    IB = T.shw[:, 128:256]
+
+    dma("Y", "drf", T.rfo[:], T.rf[:], [], ["rfo"])
+    dma("S", "ds1", T.s1[:, 0:112, :], T.sz[:], [], ["s1"])
+    dma("Y", "ds1", T.s1[:, 112:119, :], T.cd[:], [], ["s1"])
+    dma("S", "ds1", T.s1[:, 119:123, :], T.rch[:], [], ["s1"])
+    dma("Y", "ds1", T.s1[:, 123:128, :], T.sz[0:8, 0:320], [], ["s1"])
+    dma("Y", "dsz", T.szo[:], T.sz[:], [], ["szo"])
+    dma("Y", "dr1", T.r1[me, 0:112, :], T.sz[mine, :], [], ["r1"])
+    dma("Y", "dr1", T.r1[me, 112:119, :], T.cd[mine, :], [], ["r1"])
+    dma("Y", "dr1", T.r1[me, 119:123, :], T.rch[mine, :], [], ["r1"])
+    iota(T.pi[:, 0:1], [[0, 1]], 0, 1, "pi", False)
+    iota(T.ja[:], [[16, 28]], 0, 0, "ja")
+    iota(T.ion[:], [[1, S]], 0, 0, "ion")
+    iota(T.rv[:], [[0, 8], [1, 8]], 0, 0, "rv")
+    bulk_send(1)
+    iota(T.cm[:], [[0, 8], [1, 16]], 0, 0, "cm")
+    iota(T.cdv[:], [[1, 8], [0, 16]], 0, 0, "cdv")
+    iota(T.thr[:], [[0, 16], [16, 28]], W, 0, "thr")
+    for i, d in enumerate(order):
+        ms(T.gv[:, 8 * i:8 * i + 8], float(d), ["gv%d" % i])
+    GV = ["gv%d" % i for i in range(N)]
+    ts(T.pi[:, 1:2], T.pi[:, 0:1], 15, None, A.bitwise_and, None, ["pi"], ["pi1"])
+    ts(T.pi[:, 2:3], T.pi[:, 0:1], 4, None, A.arith_shift_right, None, ["pi"], ["pi2"])
+    ts(T.pi[:, 3:4], T.pi[:, 0:1], 16, None, A.bitwise_and, None, ["pi"], ["pi3"])
+    cp(T.pf[:, 0:4], T.pi[:, 0:4], ["pi", "pi1", "pi2", "pi3"], ["pf"])
+    act(PB[1][:, 0:S], T.ion[:], F.Identity, ["ion"], ["p1"], bias=float(S * me))
+    ts(T.ja[:], T.ja[:], pm, None, A.add, None, ["ja", "pf"], ["ja"])
+    ts(T.jb[:], T.ja[:], -13.5, 1.0 / 28, A.add, A.mult, ["ja"], ["jb"])
+    cp(T.ji[:], T.jb[:], ["jb"], ["ji"])
+    cp(T.jb[:], T.ji[:], ["ji"], ["jb"])
+    ts(T.jc[:], T.jb[:], -28.0, None, A.mult, None, ["jb"], ["jc"])
+    tt(T.ji[:], T.jc[:], T.ja[:], A.add, ["jc", "ja"], ["ji"])
+    ts(T.jk[:], T.ji[:], 1, None, A.bitwise_and, None, ["ji"], ["jk"])
+    ts(T.jc[:], T.jk[:], 16.0, T.pf[:, 3:4], A.mult, A.not_equal, ["jk", "pf"], ["jc"])
+    tt(T.ja[:], T.ji[:], T.jk[:], A.subtract, ["ji", "jk"], ["ja"])
+    ts(T.ja[:], T.ja[:], 16.0, T.pf[:, 3:4], A.mult, A.add, ["ja", "pf"], ["ja"])
+    ts(T.jc[:], T.jc[:], float(S), None, A.mult, None, ["jc"], ["jc"])
+    tt(T.ja[:], T.ja[:], T.jb[:], A.add, ["ja", "jb"], ["ja"])
+    tt(T.ja[:], T.ja[:], T.jc[:], A.add, ["ja", "jc"], ["ja"])
+    cp(T.pl[:], T.ja[:], ["ja"], ["pl"])
+    ts(T.pf[:, 4:5], T.pf[:, 3:4], -2.0, 16.0, A.mult, A.add, ["pf"], ["pf4"])
+    ts(T.pf[:, 4:5], T.pf[:, 4:5], pp, None, A.add, None, ["pf", "pf4"], ["pf4"])
+    ts(T.swp[:], T.ion[:, 0:128], T.pf[:, 4:5], None, A.is_equal, None, ["ion", "pf4"], ["swp"])
+    ts(T.u16[:], T.ion[:, 0:16], pd, 8.0, A.add, A.is_ge, ["ion", "pf"], ["u16"])
+    ts(T.cv[:], T.u16[:], -8.0, None, A.mult, None, ["u16"], ["cv"])
+    tt(T.cv[:], T.cv[:], T.ion[:, 0:16], A.add, ["cv", "ion"], ["cv"])
+    ts(T.cv[:], T.cv[:], 2.0, 17.0, A.mult, A.add, ["cv"], ["cv"])
+    ts(T.t16[:, 8:9], pm, 1.0, None, A.is_equal, None, ["pf"], ["t16b"])
+    ts(T.cv[:], T.cv[:], T.t16[:, 8:9], None, A.mult, None, ["cv", "t16b"], ["cv"])
+    for j in range(6):
+        act(T.jt[:, S * j:S * j + S], T.ion[:], F.Identity, ["ion", "cv"], ["jt%d" % j], scale=0.0, bias=T.cv[:, j:j + 1])
+    tt(T.ta[:], T.rfo[:], PB[1][:, 0:S], A.is_ge, ["rfo", "p1"], ["ta"])
+    ts(PB[2][:, 0:S], T.ta[:], float(-W), float(W - S * me), A.mult, A.add, ["ta"], ["p2"])
+    tt(T.lo[:], T.rfo[:], PB[2][:, 0:S], A.add, ["rfo", "p2"], ["lo"])
+    op("V", lambda: V.transpose(T.yw[:, 0:S], T.lo[:]), ["lo"], ["yw0"])
+    mm(PB[0][:, 0:S], T.swp[:], T.yw[:, 0:S], True, True, ["swp", "yw0"], "p0")
+    act(T.yw[:, S:2 * S], PB[0][:, 0:S], F.Identity, ["p0"], ["yw1"])
+    ts(T.m2[:, S:2 * S], T.rfo[:], float(W - S * me), None, A.add, None, ["rfo"], ["m2b"])
+    cp(T.szob[:], T.szo[:], ["szo"], ["szob"])
+    act(T.to[:], T.szob[:], F.Identity, ["szob"], ["to", "tot0"], accum_out=T.tot[:, 0:1])
+    ts(T.mo[:], T.rv[:], float(me), None, A.is_gt, None, ["rv"], ["mo"])
+    ts(T.t64[:], T.gv[:], pd, None, A.is_gt, None, GV + ["pf"], ["t64"])
+    ts(T.u64[:], T.rv[:], float(me), None, A.is_equal, None, ["rv"], ["u64"])
+    tt(T.t64[:], T.t64[:], T.u64[:], A.mult, ["t64", "u64"], ["t64"])
+    tt(T.mo[:], T.mo[:], T.t64[:], A.add, ["mo", "t64"], ["mo"])
+    sums_send(0, T.mo, "mo")
+    cp(T.m2[:, 0:S], T.yw[:, 0:2 * S].indirect(T.pl[:, 0:28]), ["yw0", "yw1", "pl"], ["m2a"])
+    dma("Y", "ds2", T.s2[:, 64:128, :], T.m2[:, S:2 * S], ["m2b"], ["s2"])
+    dma("Y", "ds2", T.r2[me, 64:128, :], T.m2[mine, S:2 * S], ["m2b"], ["r2"])
+    dma("S", "ds2", T.s2[:, 0:64, :], T.m2[:, 0:S], ["m2a"], ["s2"])
+    dma("S", "ds2", T.r2[me, 0:64, :], T.m2[mine, 0:S], ["m2a"], ["r2"])
+    bulk_send(2)
+    dma("Y", "ds3", T.s3[:, 119:128, :], T.ion[0:72, 0:64], ["ion"], ["s3"])
+    dma("Y", "dw1", T.szi[:], T.r1[:, 0:112, :], ["r1"], ["szi"])
+    dma("Y", "dw1b", T.rci[:], T.r1[:, 119:123, :], ["r1"], ["rci"])
+    dma("Y", "dw1b", T.cdi[:], T.r1[:, 112:119, :], ["r1"], ["cdi"])
+    dma("Y", "dw2", T.lt[:], T.r2[:, 0:64, :], ["r2"], ["lt"])
+    dma("Y", "dw2b", T.ynu[:], T.r2[:, 64:128, :], ["r2"], ["ynu"])
+    ms(T.ones[:], 1.0, ["ones"])
+    ms(T.loc[:, 0:1], -CEN, ["loc0"])
+    ts(T.shw[:, 0:128], T.ion[:, 0:128], pp, -1.0, A.is_equal, A.mult, ["ion", "pf"], ["shw0"])
+    ts(T.shw[:, 128:256], T.ion[:, 0:128], pp, None, A.is_equal, None, ["ion", "pf"], ["shw"])
+    ts(T.idf[:], T.ion[:, 0:128], pp, None, A.is_equal, None, ["ion", "pf"], ["idf"])
+    ts(T.em[:], T.cm[:], pm, None, A.is_equal, None, ["cm", "pf"], ["em"])
+    ts(T.ct[:], T.ion[:, 0:8], pd, CNEG, A.is_lt, A.mult, ["ion", "pf"], ["ct"])
+    ts(T.t16[:, 0:8], T.ion[:, 0:8], pd, CPOS, A.is_gt, A.mult, ["ion", "pf"], ["t16"])
+    ts(T.ct[:], T.ct[:], -MID, None, A.add, None, ["ct"], ["ct"])
+    tt(T.ct[:], T.ct[:], T.t16[:, 0:8], A.add, ["ct", "t16"], ["ct"])
+    for j in range(6, 9):
+        act(T.jt[:, S * j:S * j + S], T.ion[:], F.Identity, ["ion", "cv"], ["jt%d" % j], scale=0.0, bias=T.cv[:, j:j + 1])
+    ts(T.sg[:], T.u16[:], 2.0, -1.0, A.mult, A.add, ["u16"], ["sg"])
+    tt(T.pi[:, 4:5], T.pi[:, 1:2], T.pi[:, 2:3], A.add, ["pi1", "pi2"], ["pi4"])
+    ts(T.pi[:, 5:6], T.pi[:, 4:5], 7, None, A.bitwise_and, None, ["pi4"], ["pi5"])
+    cp(T.rot[:, 0:1], T.pi[:, 5:6], ["pi5"], ["rot"])
+    act(T.ibig[:], IB, F.Identity, ["shw"], ["ibig"], scale=-BIG)
+    act(T.i16[:], IB, F.Identity, ["shw"], ["i16"], scale=-16.0)
+    act(T.i32[:], IB, F.Identity, ["shw"], ["i32"], scale=32.0)
+    act(T.i1k[:], IB, F.Identity, ["shw"], ["i1k"], scale=1024.0)
+    act(T.onesb[:], T.ones[:], F.Identity, ["ones"], ["onesb"])
+    act(T.i38[:], IB, F.Identity, ["shw"], ["i38"], scale=W + 224.0)
+    act(T.nc[:], T.ion[:], F.Identity, ["ion"], ["nc"], bias=-224.0)
+    act(T.ncb[:], T.ion[:], F.Identity, ["ion"], ["ncb"], bias=-224.0)
+    ms(T.kv[:], BIG + K + CEN, ["kv"])
+    ts(T.pf[:, 5:6], pd, 16.0, 15.0, A.mult, A.add, ["pf"], ["pf5"])
+    ts(T.uw[:], T.ion[:, 0:144], T.pf[:, 5:6], None, A.is_equal, None, ["ion", "pf5"], ["uw"])
+
+    def late_constants():
+        ts(T.pf[:, 6:7], pm, 0.0, None, A.is_equal, None, ["pf"], ["pf6"])
+        ts(T.pf[:, 7:8], pm, 1.0, None, A.is_equal, None, ["pf"], ["pf7"])
+        ts(T.pf[:, 8:9], T.pf[:, 7:8], 224.0, T.pf[:, 6:7], A.mult, A.add, ["pf6", "pf7"], ["pf8"])
+        ts(T.ww[:], T.uw[:], T.pf[:, 8:9], None, A.mult, None, ["uw", "pf8"], ["ww"])
+        ts(T.b20[:], T.cdv[:], pd, 20.0, A.is_equal, A.mult, ["cdv", "pf"], ["b20"])
+        ts(T.b512[:], T.cdv[:], pd, 512.0, A.is_equal, A.mult, ["cdv", "pf"], ["b512"])
+        ts(T.rep[:], T.cdv[:], pp, 1024.0, A.is_equal, A.mult, ["cdv", "pf"], ["rep"])
+        ts(T.mw[:], T.rv[:], pd, None, A.is_gt, None, ["rv", "pf"], ["mw"])
+        ts(T.t64[:], T.gv[:], float(me), None, A.is_gt, None, GV, ["t64"])
+        ts(T.u64[:], T.rv[:], pd, None, A.is_equal, None, ["rv", "pf"], ["u64"])
+        tt(T.t64[:], T.t64[:], T.u64[:], A.mult, ["t64", "u64"], ["t64"])
+        tt(T.mw[:], T.mw[:], T.t64[:], A.add, ["mw", "t64"], ["mw"])
+        ts(T.mf[:], T.gv[:], pd, None, A.is_gt, None, GV + ["pf"], ["mf"])
+        ts(T.mf[:, 1:64:8], T.gv[:, 1:64:8], pd, None, A.is_equal, None, GV + ["pf", "mf"], ["mf"])
+        act(T.ez[:, 0:128], T.em[:], F.Identity, ["em"], ["ez0"], scale=0.0)
+        act(T.ez[:, 128:256], T.em[:], F.Identity, ["em"], ["ez"])
+        ts(T.pf[:, 9:10], pd, float(S), float(-W), A.mult, A.add, ["pf"], ["pf9"])
+        ts(T.pf[:, 10:11], pd, float(S), 224.0, A.mult, A.add, ["pf"], ["pf10"])
+
+    act(T.thr[:], T.thr[:], F.Identity, ["thr", "pf"], ["thr"], bias=pm)
+    late_constants()
+    JT = ["jt%d" % j for j in range(9)]
+    TAB = ["tab%d" % j for j in range(9)]
+
+    def base_near(b):
+        mm(PB[b][:, S:S + 8], T.idf[:], T.ct[:], True, False, ["idf", "ct"], "p%d" % b)
+
+    def base_far(t, b):
+        o = 64 * t
+        tt(T.t64[:, 0:32], T.xr[:, o:o + 32], T.xr[:, o + 32:o + 64], A.add, ["xr%d" % t, "xo%d" % t], ["t64"])
+        tt(T.u64[:, 0:16], T.t64[:, 0:16], T.t64[:, 16:32], A.add, ["t64"], ["u64"])
+        tt(T.t64[:, 0:8], T.u64[:, 0:8], T.u64[:, 8:16], A.add, ["u64"], ["t64"])
+        mm(PB[b][:, S:S + 8], T.em[:], T.t64[:, 0:8], False, True, ["em", "t64"], "p%d" % b)
+
+    def rename(e, a, b):
+        src = T.jt[:, 0:9 * S].indirect(T.lt[:, 32 * a:32 * b])
+        out = T.gr[:, 512 * a:512 * b]
+        keys = ["gr%d" % u for u in range(a, b)]
+        if e == "V":
+            cp(out, src, JT + ["lt"], keys)
+        else:
+            act(out, src, F.Identity, JT + ["lt"], keys)
+
+    def turn(a, b):
+        for q in range(16):
+            mm(PB[0][:, 32 * a:32 * b], T.ww[:, 15 - q:143 - q], T.gr[:, 512 * a + q:512 * b:16], q == 0, q == 15,
+               ["ww"] + ["gr%d" % u for u in range(a, b)], "p0", q == 15)
+
+    def empty(e, j):
+        out = T.tab[:, S * j:S * j + S]
+        if e == "V":
+            ts(out, PB[j][:, 0:S], T.cs[:, j:j + 1], None, A.add, None, ["p%d" % j, "cs"], ["tab%d" % j])
+        else:
+            act(out, PB[j][:, 0:S], F.Identity, ["p%d" % j, "cs"], ["tab%d" % j], bias=T.cs[:, j:j + 1])
+
+    def lengths(t):
+        far = T.far[:, S * (t % 2):S * (t % 2) + S]
+        ts(far, PB[2][:, 0:S], 0.0, None, A.not_equal, None, ["p2"], ["far%d" % (t % 2)])
+        if t == RO:
+            dma("Y", "ds4", T.s4[:], far, ["far0"], ["s4"])
+            dma("Y", "ds4", T.r4[me], T.far[mine, 0:S], ["far0"], ["r4"])
+        mm(PB[5][:, 0:S], T.b20[:], far, False, True, ["b20", "far%d" % (t % 2)], "p5")
+        act(T.ln[:], PB[5][:, 0:S], F.Relu, ["p5"], ["ln", "tot%d" % t], bias=-1024.0, accum_out=T.tot[:, t:t + 1])
+
+    def gap(t):
+        ren = t > 0
+        if ren:
+            rename("S", 1, 3)
+            lengths(t)
+            sums_send(t, T.mw, "mw")
+            rename("V", 0, 1)
+            turn(0, 3)
+            rename("S", 3, 6)
+            src, sk = T.ln, "ln"
+        else:
+            cp(T.szb[:], T.szi[:], ["szi"], ["szb"])
+            src, sk = T.szb, "szb"
+        op("V", lambda: V.tensor_tensor_scan(T.loc[:, 1:S], T.ones[:, 0:S - 1], src[:, 0:S - 1], -CEN, A.mult, A.add), ["ones", sk], ["loc"])
+        cp(T.hi[:], T.loc[:], ["loc", "loc0"], ["hi"])
+        tt(T.lw[:], T.loc[:], T.hi[:], A.subtract, ["loc", "loc0", "hi"], ["lw"])
+        def own():
+            act(T.tab[:, 0:S], T.loc[:], F.Identity, ["loc", "loc0"], ["tab0"], scale=-1.0, bias=-CPOS)
+            act(T.tab[:, 8 * S:9 * S], T.loc[:], F.Identity, ["loc", "loc0"], ["tab8"], bias=CNEG)
+
+        if not ren:
+            own()
+            ts(T.bk[:], T.rci[:], -0.5 * K, None, A.add, None, ["rci"], ["bk"])
+            base_near(0)
+        js = [7, 1, 5, 2, 6, 3, 4]
+        for j in js[:4]:
+            mm(PB[j][:, 0:S], T.shw[:, 16 * j:16 * j + 128], T.hi[:], True, False, ["shw", "shw0", "hi"], "p%d" % j)
+        if not ren:
+            base_far(t, 0)
+        for j in js:
+            if j not in js[:4]:
+                mm(PB[j][:, 0:S], T.shw[:, 16 * j:16 * j + 128], T.hi[:], True, False, ["shw", "shw0", "hi"], "p%d" % j)
+            mm(PB[j][:, 0:S], T.shw[:, 16 * j:16 * j + 128], T.lw[:], False, True, ["shw", "shw0", "lw"], "p%d" % j)
+        if ren:
+            rename("V", 6, 9)
+            rename("S", 9, 12)
+            rename("V", 12, 14)
+            own()
+            base_near(7)
+            turn(3, 6)
+            turn(6, 9)
+            turn(9, 12)
+            base_far(t, 7)
+            turn(12, 14)
+        bb = 7 if ren else 0
+        cp(T.bs[:], PB[bb][:, S:S + 8], ["p%d" % bb], ["bs"])
+        cp(T.ro[:], T.bs[:, 0:8].indirect(T.rot[:, 0:1]), ["bs", "rot"], ["ro"])
+        ts(T.c1[:], T.ro[:], T.ro[:, 0:1], CPOS, A.subtract, A.max, ["ro"], ["c1"])
+        tt(T.cs[:], T.c1[:], T.sg[:], A.mult, ["c1", "sg"], ["cs"])
+        al = T.al[:, S * (t % 2):S * (t % 2) + S] if ren else T.onesb[:]
+        ak = "al%d" % (t % 2) if ren else "onesb"
+        empty("V", 1)
+        empty("S", 7)
+        mm(PB[1][:, 0:S], T.kv[0:1, :], T.onesb[0:1, :], True, False, ["kv", "onesb"], "p1")
+        mm(PB[1][:, 0:S], T.ibig[:], al, False, False, ["ibig", ak], "p1")
+        mm(PB[1][:, 0:S], IB, T.hi[:], False, False, ["shw", "hi"], "p1")
+        mm(PB[1][:, 0:S], IB, T.lw[:], False, True, ["shw", "lw"], "p1")
+        if ren:
+            tt(T.ta[:], PB[0][:, 0:S], T.thr[:], A.is_ge, ["p0", "thr"], ["ta"])
+            ts(T.tb[:], T.ta[:], float(-W), None, A.mult, None, ["ta"], ["tb"])
+            tt(T.tc[:], PB[0][:, 0:S], T.tb[:], A.add, ["p0", "tb"], ["tc"])
+        empty("S" if ren else "V", 2)
+        empty("S", 5)
+        empty("S", 6)
+        empty("V", 3)
+        empty("S" if ren else "V", 4)
+        if ren:
+            cp(T.lt[:], T.tc[:], ["tc"], ["lt"])
+        else:
+            cp(T.cdl[:], T.cdi[:], ["cdi"], ["cdl"])
+            cp(T.cb[:], T.nc[:, 0:S].indirect(T.cdl[:, 0:28]), ["nc", "cdl"], ["cb"])
+
+    def main(t):
+        al = T.al[:, S * (t % 2):S * (t % 2) + S]
+        ak = "al%d" % (t % 2)
+        GR = ["gr%d" % c for c in range(14)]
+
+        def side0():
+            if t == 1:
+                cp(T.ref[:], T.ynu[:], ["ynu"], ["ref"])
+                cp(T.nth[:], T.ynu[:], ["ynu"], ["nth"])
+            else:
+                for k in range(16):
+                    mm(PB[3][:, 0:S], T.ww[:, 15 - k:143 - k], T.gr[:, S * k:S * k + S], k == 0, k == 15, ["ww"] + GR, "p3")
+
+        def side1():
+            if t > 1:
+                cp(T.ref[:], PB[3][:, 0:S], ["p3"], ["ref"])
+                cp(T.nth[:], PB[3][:, 0:S], ["p3"], ["nth"])
+            was = T.al[:, S * ((t - 1) % 2):S * ((t - 1) % 2) + S] if t > 1 else T.onesb[:]
+            mm(PB[6][:, 0:S], IB, T.ncb[:], True, False, ["shw", "ncb"], "p6")
+            mm(PB[6][:, 0:S], T.i38[:], was, False, True, ["i38", "al%d" % ((t - 1) % 2) if t > 1 else "onesb"], "p6")
+            mm(PB[4][:, 0:S], IB, T.cb[:], True, False, ["shw", "cb"], "p4")
+
+        def side2():
+            tt(T.mis[:], T.ref[:, 0:S].indirect(T.cdl[:, 0:28]), T.nth[:], A.not_equal, ["ref", "nth", "cdl"], ["mis"])
+            mm(PB[4][:, 0:S], T.b512[:], T.mis[:], False, True, ["b512", "mis"], "p4")
+
+        def side3():
+            tt(T.neg[:], T.ref[:], PB[6][:, 0:S], A.is_lt, ["ref", "p6"], ["neg"])
+            mm(PB[2][:, 0:S], T.i16[:], T.neg[:], False, False, ["i16", "neg"], "p2")
+
+        def side4():
+            if t < RO:
+                tt(T.jv[:], PB[4][:, 0:S], T.nc[:], A.min, ["p4", "nc"], ["jv"])
+                for j in range(9):
+                    a = j % 8
+                    dma("Y", "dj%d" % (t - 1), T.jt[0:128 - 16 * a:16, S * j:S * j + S], T.jv[16 * a:128:16, :], ["jv"], ["jt%d" % j])
+                    if a:
+                        dma("Y", "dj%d" % (t - 1), T.jt[128 - 16 * a:128:16, S * j:S * j + S], T.jv[0:16 * a:16, :], ["jv"], ["jt%d" % j])
+            else:
+                tt(T.tc[:], PB[4][:, 0:S], T.nc[:], A.min, ["p4", "nc"], ["tc"])
+                ts(T.yjf[:], T.tc[:], T.pf[:, 10:11], None, A.add, None, ["tc", "pf10"], ["yjf"])
+                ts(T.yrf[:], T.ref[:], T.pf[:, 9:10], None, A.add, None, ["ref", "pf9"], ["yrf"])
+                dma("Y", "ds3", T.s3[:, 0:112, :], T.yrf[:], ["yrf"], ["s3"])
+                dma("Y", "ds3", T.s3[:, 112:119, :], T.yjf[0:128:16, :], ["yjf"], ["s3"])
+                dma("Y", "ds3", T.r3[me, 0:112, :], T.yrf[mine, :], ["yrf"], ["r3"])
+                dma("Y", "ds3", T.r3[me, 112:119, :], T.yjf[16 * me:16 * me + 1, :], ["yjf"], ["r3"])
+                bulk_send(3)
+
+        def side5():
+            tt(al, PB[4][:, 0:S], T.nc[:], A.is_ge, ["p4", "nc"], [ak])
+            mm(PB[5][:, 0:S], IB, T.szb[:], True, False, ["shw", "szb"], "p5")
+            mm(PB[5][:, 0:S], T.i1k[:], al, False, False, ["i1k", ak], "p5")
+
+        side = {0: side0, 3: side1, 4: side2, 5: side4, 7: side3, 9: side5}
+        for k in range(16):
+            act(T.gg[:, S * k:S * k + S], T.tab[:, 0:9 * S].indirect(T.lt[:, 28 * k:28 * k + 28]), F.Abs, TAB + ["lt", "bk"], ["gg%d" % k], bias=T.bk[:, k:k + 1])
+            if k == 0 and t > 1:
+                side0()
+            tt(T.ind[:, S * k:S * k + S], T.gg[:, S * k:S * k + S], PB[1][:, 0:S], A.is_gt, ["gg%d" % k, "p1"], ["ind%d" % k])
+            mm(PB[2][:, 0:S], T.uw[:, 15 - k:143 - k], T.ind[:, S * k:S * k + S], k == 0, k == 15, ["uw", "ind%d" % k], "p2")
+            if k == 0 and t > 1:
+                o = S * ((t - 1) % 2)
+                mm(PB[2][:, 0:S], T.i32[:], T.far[:, o:o + S], False, False, ["i32", "far%d" % ((t - 1) % 2)], "p2")
+            if k in side and not (k == 0 and t > 1):
+                side[k]()
+
+    for t in range(RO):
+        gap(t)
+        main(t + 1)
+
+    lengths(RO)
+    sums_send(RO, T.mf, "mf")
+    bulk_send(4)
+    dma("Y", "do3", T.jrow[0:8, :], T.r3[:, 112:119, :], ["r3"], ["jrow"])
+    dma("Y", "do4", T.faro[:], T.r4[:], ["r4"], ["faro"])
+    dma("S", "dy", T.yr[:], T.r3[:, 0:112, :], ["r3"], ["yr"])
+    dma("S", "dy", T.yj[:], T.r3[:, 112:119, :], ["r3"], ["yj"])
+    ts(T.yjf[0:8, :], T.jrow[0:8, :], float(-S * me), None, A.add, None, ["jrow"], ["yjf"])
+    tt(T.al8[0:8, :], T.yjf[0:8, :], T.ion[0:8, :], A.is_equal, ["yjf", "ion"], ["al8"])
+    mm(PB[6][:, 0:S], IB, T.szob[:], True, False, ["shw", "szob"], "p6")
+    mm(PB[6][:, 0:S], T.rep[0:8, :], T.al8[0:8, :], False, False, ["rep", "al8"], "p6")
+    for q in order[::-1]:
+        src, o, k = (T.xs, 64 * RO + 8 * order.index(me), "xs") if q == me else (T.xr, 64 * RO + 8 * q, "xr")
+        mm(PB[7][:, 0:1], T.em[:], src[:, o:o + 1], q == me, False, ["em", k + str(RO)], "p7")
+        mm(PB[7][:, 0:1], T.ez[:, 112 - 16 * q:240 - 16 * q], src[:, o + 1:o + 2], False, q == order[0], ["ez", "ez0", k + str(RO)], "p7")
+    cp(T.yaf[:, 0:1], PB[7][:, 0:1], ["p7"], ["yaf0"])
+    mm(PB[6][:, 0:S], T.b20[:], T.faro[:], False, True, ["b20", "faro"], "p6")
+    act(T.ln[:], PB[6][:, 0:S], F.Relu, ["p6"], ["ln"], bias=-1024.0)
+    dma("G", "dg", T.yf[:], T.r4[:], ["r4"], ["yf"])
+    op("V", lambda: V.tensor_tensor_scan(T.yaf[:, 1:S], T.ones[:, 0:S - 1], T.ln[:, 0:S - 1], T.yaf[:, 0:1], A.mult, A.add), ["ones", "ln", "yaf0"], ["yaf"])
+    dma("Y", "dy", T.ya[:], T.yaf[:], ["yaf", "yaf0"], ["ya"])
+    for s in cnt:
+        need("G", (s, None))

@@ -1,5 +1,5 @@
 from concourse.bass import DstId, RemoteDMATransfer
-from concourse.mybir import AluOpType as A, ActivationFunctionType as F
+from concourse.mybir import AluOpType as A, ActivationFunctionType as F, AxisListType as AX
 
 N, S, RO = 8, 448, 4
 W = N * S
@@ -8,40 +8,52 @@ K = 8781824.0
 CPOS = 0.5 * K + CEN
 CNEG = 1.5 * K + 1 + CEN
 MID = 13800000.0
-BIG = 67108864.0
-CH = 7
+BIG = 33554432.0
+MAG = 192.0
+C0 = S * MAG - W - 224
+NA = 3
+Q4 = S // 4
+PARTS = [(0, 3), (3, 10), (10, 16)]
+PARTS0 = [(0, 5), (5, 10), (10, 16)]
+BB = 6
+CY, GAT = 0.00083, 1.56
+XL, PASSES = 5.0, 6
 
 SB = lambda n, d="float32": ("sbuf", [128, n], d)
+H = "bfloat16"
 SCRATCH = {
-    "s1": ("dram", [N, 128, 64], "int32"), "r1": ("dram", [N, 128, 64], "int32"),
-    "s2": ("dram", [N, 128, 112], "uint16"), "r2": ("dram", [N, 128, 112], "uint16"),
+    "s0": ("dram", [N, 128, 8], "int32"), "r0": ("dram", [N, 128, 8], "int32"),
+    "s1": ("dram", [N, 128, 56], H), "r1": ("dram", [N, 128, 56], H),
+    "s5": ("dram", [N, 128, 112], H), "r5": ("dram", [N, 128, 112], H),
+    "s2": ("dram", [N, 128, 112], H), "r2": ("dram", [N, 128, 112], H),
     "s3": ("dram", [N, 128, 64], "float32"), "r3": ("dram", [N, 128, 64], "float32"),
-    "s4": ("dram", [N, 128, 56], "bfloat16"), "r4": ("dram", [N, 128, 56], "bfloat16"),
+    "s4": ("dram", [N, 128, 56], H), "r4": ("dram", [N, 128, 56], H),
     "xs": SB(5 * 64), "xr": SB(5 * 64),
-    "pi": SB(8, "int32"), "pf": SB(16), "ion": SB(S), "nc": SB(S), "ncb": SB(S, "bfloat16"), "i38": SB(128, "bfloat16"), "i35": SB(128, "bfloat16"), "zr": SB(128, "bfloat16"), "ez": SB(256), "thr": SB(S), "ones": SB(S),
-    "onesb": SB(S, "bfloat16"), "kv": SB(128, "bfloat16"), "cm": SB(128), "cdv": SB(128), "rv": SB(64), "gv": SB(64),
-    "mw": SB(64), "mo": SB(64), "mf": SB(64), "t64": SB(64), "u64": SB(64),
-    "shw": SB(256, "bfloat16"), "i1k": SB(128, "bfloat16"), "ibig": SB(128, "bfloat16"), "i16": SB(128, "bfloat16"),
-    "i32": SB(128, "bfloat16"), "idf": SB(128), "swp": SB(128), "ww": SB(144, "bfloat16"), "uw": SB(144, "bfloat16"),
-    "b20": SB(128, "bfloat16"), "b512": SB(128, "bfloat16"), "em": SB(128), "lm": SB(128), "rep": SB(128, "bfloat16"),
-    "ct": SB(8), "sg": SB(16), "cv": SB(16), "t16": SB(16), "u16": SB(16), "rot": SB(2, "uint16"),
-    "ja": SB(28), "jb": SB(28), "jc": SB(28), "ji": SB(28, "int32"), "jk": SB(28, "int32"), "pl": SB(28, "uint16"),
-    "szo": SB(S, "int32"), "rfo": SB(S, "int32"), "szob": SB(S, "bfloat16"), "yo": SB(S), "to": SB(S), "lo": SB(S),
-    "yw": SB(2 * S), "m2": SB(2 * S, "uint16"), "jrow": SB(S), "al8": SB(S, "bfloat16"), "faro": SB(S, "bfloat16"),
-    "yff": SB(S), "yaf": SB(S),
-    "szi": SB(S, "int32"), "cdi": SB(28, "int32"), "rci": SB(16, "int32"), "szb": SB(S, "bfloat16"),
-    "cdl": SB(28, "uint16"), "bk": SB(16), "cb": SB(S, "bfloat16"), "lt": SB(S, "uint16"), "ynu": SB(S, "uint16"),
-    "ln": SB(S), "tot": SB(8), "loc": SB(S), "hi": SB(S, "bfloat16"), "lw": SB(S, "bfloat16"),
-    "tab": SB(9 * S), "jt": SB(9 * S, "bfloat16"), "gr": SB(16 * S, "bfloat16"), "gg": SB(16 * S),
-    "ind": SB(16 * S, "bfloat16"), "bs": SB(8), "ro": SB(16), "c1": SB(16), "cs": SB(16),
-    "ta": SB(S, "bfloat16"), "tb": SB(S, "bfloat16"), "tc": SB(S),
-    "ref": SB(S), "neg": SB(S, "bfloat16"), "mis": SB(S, "bfloat16"), "al": SB(2 * S, "bfloat16"), "jv": SB(S, "bfloat16"),
-    "nth": SB(S), "far": SB(2 * S, "bfloat16"), "yrf": SB(S), "yjf": SB(S),
+    "pi": SB(8, "int32"), "pf": SB(24), "ion": SB(S), "nc": SB(S), "ncb": SB(S, H), "tb": SB(S, H), "thr": SB(S), "ones": SB(S),
+    "onesb": SB(S, H), "kv": SB(128, H), "cm": SB(128), "cdv": SB(128), "rv": SB(64), "gv": SB(64),
+    "mw": SB(64), "mo": SB(64), "t64": SB(64), "u64": SB(64),
+    "shw": SB(256, H), "ip": SB(128, H), "im": SB(128, H), "i16": SB(128, H), "i32": SB(128, H), "iw": SB(128, H),
+    "nf": SB(128, H), "i448": SB(128, H), "na": SB(128, H), "nb": SB(128, H), "nd": SB(128, H), "ne": SB(128, H),
+    "idf": SB(128), "ww": SB(144, H), "w1": SB(144, H), "uw": SB(144, H), "nlc": SB(28 * NA + 16, H),
+    "b20": SB(128, H), "b512": SB(128, H), "em": SB(128), "ema": SB(128), "emb": SB(128), "rep": SB(128, H),
+    "ct": SB(8), "sg": SB(16), "cv": SB(16), "t16": SB(16), "u16": SB(16), "mk": SB(16), "rot": SB(2, "uint16"),
+    "d20": SB(8, H), "d64": SB(8, H), "d65": SB(8, H), "xf": SB(32), "xl": SB(32, "uint16"),
+    "szo": SB(S, "int32"), "rfo": SB(S, "int32"), "szob": SB(S, H), "to": SB(S), "m2": SB(2 * S, H), "jrow": SB(S),
+    "al8": SB(S, H), "szal": SB(S, H), "xe": SB(512, H), "yaf": SB(S),
+    "cdo": SB(28, "int32"), "cdm": SB(28, "uint16"), "m5": SB(2 * S, H), "m6": SB(2 * S, H), "nth": SB(S, H), "cbo": SB(S, H), "sm": SB(S, H),
+    "cdi": SB(28, "int32"), "rci": SB(16, "int32"), "szb": SB(S + 16, H),
+    "cdl": SB(28, "uint16"), "bk": SB(16), "cb": SB(S, H), "lt": SB(S, "uint16"), "ol": SB(28 * NA + 16, "uint16"),
+    "ln": SB(S + 8), "tot": SB(8), "hi": SB(S, H), "lw": SB(S, H), "g1": SB(16 * S, H),
+    "tab": SB(9 * S), "jt": SB(9 * S, H), "gr": SB(16 * S, H), "gg": SB(16 * S), "ind": SB(16 * S, H),
+    "bs": SB(8), "ro": SB(16), "c1": SB(16), "cs": SB(16), "ta": SB(S, H), "tc": SB(S),
+    "ref": SB(S, H), "sl": SB(S, H), "neg": SB(S, H), "mis": SB(S, H),
+    "jv": SB(2 * S, H), "far": SB(2 * S, H), "yrf": SB(S), "yjf": SB(S),
 }
 for _b in range(8):
     SCRATCH["p%d" % _b] = ("psum", [128, 512], "float32")
-SEMAPHORES = (["cV", "cS", "cP", "cG", "out", "m1", "m2", "m3", "m4", "dg"] + ["xr%d" % t for t in range(5)]
-              + ["dsz", "drf", "ds1", "dr1", "dw1", "dw1b", "ds2", "dw2", "dw2b", "dj0", "dj1", "dj2", "ds3", "do3", "dy", "ds4", "do4"])
+SEMAPHORES = (["cV", "cS", "cP", "cG", "out", "dg"] + ["m%d" % i for i in range(6)] + ["xr%d" % t for t in range(5)]
+              + ["dsz", "drf", "dcd", "ds0", "dr0", "ds5", "dw5", "ds1", "dw1", "dw1b", "ds2", "dw2", "dw2b", "dj0", "dj1", "dj2",
+                 "dn0", "dn1", "dn2", "ds3", "do3", "dy", "dz", "ds4"])
 
 
 def plan(T, topo, r):
@@ -83,7 +95,7 @@ def split(T, topo, r):
     return off, on
 
 
-ORDER = ["m1", "x0", "m2", "x1", "x2", "x3", "m3", "x4", "m4"]
+ORDER = ["m0", "m1", "m2", "x0", "m5", "x1", "x2", "x3", "m3", "x4", "m4"]
 
 
 def helper(g, core, T, topo):
@@ -123,6 +135,8 @@ def rank_program(g, core, T, topo):
     off, on = split(T, topo, me)
     order = away + direct + [me]
     Q = {"V": g.vector, "S": g.scalar, "P": g.tensor, "G": g, "Y": g.sync}
+    V, Sc, P = g.vector, g.scalar, g.tensor
+
     cnt, seen, wr, rd = {}, {}, {}, {}
 
     def need(e, tok):
@@ -157,7 +171,7 @@ def rank_program(g, core, T, topo):
             if not add:
                 rd[k] = {}
 
-    def op(e, fn, reads, writes, inc=True):
+    def op_now(e, fn, reads, writes, inc=True):
         deps(e, reads, writes)
         ins = fn()
         s = "c" + e
@@ -168,7 +182,7 @@ def rank_program(g, core, T, topo):
         else:
             note(e, (s, cnt.get(s, 0) + 1), reads, writes)
 
-    def dma(e, sem, out, in_, reads, writes):
+    def dma_now(e, sem, out, in_, reads, writes):
         fresh = [k for k in writes if (sem, None) not in wr.get(k, [])]
         deps(e, reads, fresh)
         Q[e].dma_start(out, in_).then_inc(T.sem[sem], 16)
@@ -184,7 +198,7 @@ def rank_program(g, core, T, topo):
         g.remote_dma_fused(xs, local_sem=T.sem.out)
         cnt["out"] = cnt.get("out", 0) + n
 
-    def bulk_send(i):
+    def bulk_now(i):
         s, r, sem = T["s%d" % i], T["r%d" % i], "m%d" % i
         ea, eb = share(off, len(direct)), share(on, len(away))
         xs = [xfer(topo, core, bulk[d], s[d], r[d], e, T.sem[sem]) for d, e in zip(away, eb)]
@@ -200,17 +214,14 @@ def rank_program(g, core, T, topo):
                     n += len(share(topo.engines(bq[me], core), sum(1 for d in aq if bq[d] == bq[me]))[0])
         arrive(sem, n, "r%d" % i, True)
 
-    def sums_send(t, mask, mk):
-        op("S", lambda: g.scalar.activation(T.xs[:, 64 * t:64 * t + 64], mask[:], F.Identity, scale=T.tot[:, t:t + 1]), [mk, "tot%d" % t], ["xs%d" % t])
-        if t < RO:
-            act(T.xr[:, 64 * t + 8 * me:64 * t + 8 * me + 8], mask[:, 56:64], F.Identity, [mk, "tot%d" % t], ["xo%d" % t], scale=T.tot[:, t:t + 1])
+    def small_now(t, reads):
         eb = share(on + off, len(small))
-        wide = 64 // len(small)
+        cols = 64 // len(small)
         xs = []
         for (c, ds), e in zip(small, eb):
             o = 64 * t + 8 * order.index(ds[0])
-            xs.append(xfer(topo, core, c, T.xs[:, o:o + wide], T.xs[:, 64 * t:64 * t + wide], e, T.sem["xr%d" % t]))
-        fused(xs, ["xs%d" % t], sum(len(e) for e in eb))
+            xs.append(xfer(topo, core, c, T.xs[:, o:o + cols], T.xs[:, 64 * t:64 * t + cols], e, T.sem["xr%d" % t]))
+        fused(xs, reads, sum(len(e) for e in eb))
         nr = 0
         for q in range(N):
             if q != me:
@@ -218,372 +229,462 @@ def rank_program(g, core, T, topo):
                 nr += len(share(topo.engines(c, core), len(ds))[0])
         arrive("xr%d" % t, nr, "xr%d" % t)
 
-    V, Sc, P = g.vector, g.scalar, g.tensor
+    nodes, lastw, readers, held, batch, mates = [], {}, {}, {}, {}, {}
+    wide = [S]
 
-    def ts(out, in0, s1, s2, o0, o1, reads, writes):
+    def node(engs, fn, reads, writes, dur, lat=0.0, adds=()):
+        i = len(nodes)
+        pre = set()
+        for k in reads:
+            pre.update(lastw.get(k, []))
+            if k[0] == "p" and k[1:].isdigit():
+                pre.update(j for j in readers.get(k, []) if nodes[j][0] != engs or len(engs) > 1)
+        for k in list(writes) + list(adds):
+            pre.update(readers.get(k, []))
+            pre.update(j for j in lastw.get(k, []) if k in writes or k not in nodes[j][5])
+        for k in reads:
+            readers.setdefault(k, []).append(i)
+        for k in writes:
+            lastw[k], readers[k] = [i], []
+        for k in adds:
+            if readers.get(k) or not all(k in nodes[j][5] for j in lastw.get(k, [])):
+                held[k] = set(readers.get(k, [])) | set(lastw.get(k, []))
+                lastw[k], readers[k] = [], []
+            pre.update(held.get(k, ()))
+            lastw.setdefault(k, []).append(i)
+        for j in list(pre):
+            pre.update(mates.get(j, ()))
+        pre.discard(i)
+        nodes.append((engs, fn, pre, dur, lat, set(adds)))
+
+    def op(e, fn, reads, writes, n=None, per=1.0):
+        n = wide[0] if n is None else n
+        fix = {"V": 0.05, "S": 0.065, "G": 0.13}
+        node(e, lambda x: op_now(x, fn if len(e) == 1 else (lambda: fn(x)), reads, writes), reads, writes,
+             {x: fix[x] + max(n * per, 16) * CY for x in e}, 0.06)
+
+    def dma(e, sem, out, in_, reads, writes, lat=1.9, now=False):
+        if now:
+            dma_now(e, sem, out, in_, reads, writes)
+            node("", None, reads, [], {}, lat, adds=list(writes))
+        else:
+            node(e, lambda x: dma_now(e, sem, out, in_, reads, writes), reads, [], {e: 0.06 if e != "G" else 1.5}, lat, adds=list(writes))
+        batch.setdefault(sem, []).append(len(nodes) - 1)
+        mates[len(nodes) - 1] = batch[sem]
+
+    def remote(fn, reads, key, lat):
+        first = "gq" not in lastw
+        node("G", lambda x: fn(), reads, ["gq", "sent" + key], {"G": 2.8 if first else 0.6}, 0.0)
+        node("", None, ["sent" + key], [], {}, lat + (2.4 if first else 0), adds=[key])
+
+    def mms(calls, bank, adds=False):
+        reads = sorted({k for c in calls for k in c[5]})
+
+        def now(x):
+            for j, (out, l, r, st, sp, ks, n) in enumerate(calls):
+                if adds:
+                    st, sp = adds()
+                op_now("P", lambda: P.matmul(out, l, r, st, sp), ks, [bank], j == len(calls) - 1)
+        node("P", now, reads, [] if adds else [bank], {"P": sum(max(64, c[6]) for c in calls) * CY / 2}, 0.12, adds=[bank] if adds else [])
+
+    def issue():
+        n = len(nodes)
+        pre = [nd[2] for nd in nodes]
+        post = [[] for _ in range(n)]
+        for i in range(n):
+            for j in pre[i]:
+                post[j].append(i)
+
+        def lay(seq, before, back):
+            busy = {x: [] for x in "VSPGY"}
+            fin, start, eng = [0.0] * n, [0.0] * n, [""] * n
+            for i in seq:
+                engs, fn, _, dur, lat, _ = nodes[i]
+                r = max((fin[j] for j in before[i]), default=0.0) + (lat if back else 0.0)
+                best = (r, r, "", 0)
+                for x in engs:
+                    t, at = r, len(busy[x])
+                    while at and busy[x][at - 1][1] > t:
+                        at -= 1
+                    while at < len(busy[x]) and busy[x][at][0] < t + dur[x]:
+                        t = max(t, busy[x][at][1])
+                        at += 1
+                    if not best[2] or t + dur[x] < best[1]:
+                        best = (t, t + dur[x], x, at)
+                start[i], end, eng[i], at = best
+                if eng[i]:
+                    busy[eng[i]].insert(at, (start[i], end))
+                fin[i] = end + (0.0 if back else lat)
+            return fin, start, eng
+
+        seq, kept = list(range(n)), None
+        for _ in range(PASSES):
+            fin, start, eng = lay(seq, pre, False)
+            if kept is None or max(fin) < kept[0]:
+                kept = (max(fin), start, eng)
+            fin = lay(sorted(range(n), key=lambda i: (-fin[i], -i)), post, True)[0]
+            seq = sorted(range(n), key=lambda i: (-fin[i], i))
+        for i in sorted(range(n), key=lambda i: (kept[1][i], i)):
+            if kept[2][i]:
+                nodes[i][1](kept[2][i])
+
+    def bulk_send(i):
+        remote(lambda: bulk_now(i), ["s%d" % i], "r%d" % i, XL + 0.5)
+
+    def small_send(t, reads):
+        remote(lambda: small_now(t, reads), reads, "xr%d" % t, XL + (1.0 if t == 0 else 0.0))
+
+    def sums_send(t, mask, mk):
+        act(T.xs[:, 64 * t:64 * t + 64], mask[:], F.Identity, [mk, "tot%d" % t], ["xs%d" % t], 64, scale=T.tot[:, t:t + 1])
+        small_send(t, ["xs%d" % t])
+        lin(T.xr[:, 64 * t + 8 * me:64 * t + 8 * me + 8], mask[:, 56:64], T.tot[:, t:t + 1], 0.0, [mk, "tot%d" % t], ["xo%d" % t], 16)
+
+    def ts(out, in0, s1, s2, o0, o1, reads, writes, n=None, per=1.0):
         if o1 is None:
-            op("V", lambda: V.tensor_scalar(out, in0, s1, None, o0), reads, writes)
+            op("V", lambda: V.tensor_scalar(out, in0, s1, None, o0), reads, writes, n, per)
         else:
-            op("V", lambda: V.tensor_scalar(out, in0, s1, s2, o0, o1), reads, writes)
+            op("V", lambda: V.tensor_scalar(out, in0, s1, s2, o0, o1), reads, writes, n, per)
 
-    def tt(out, a, b, o, reads, writes):
-        op("V", lambda: V.tensor_tensor(out, a, b, o), reads, writes)
+    def tt(out, a, b, o, reads, writes, n=None, per=1.0):
+        op("V", lambda: V.tensor_tensor(out, a, b, o), reads, writes, n, per)
 
-    def cp(out, a, reads, writes):
-        op("V", lambda: V.tensor_copy(out, a), reads, writes)
+    def cp(out, a, reads, writes, n=None, per=1.0):
+        op("V", lambda: V.tensor_copy(out, a), reads, writes, n, per)
 
-    def ms(out, v, writes):
-        op("V", lambda: V.memset(out, v), [], writes)
+    def ms(out, v, writes, n=None):
+        op("V", lambda: V.memset(out, v), [], writes, n)
 
-    def act(out, a, f, reads, writes, **kw):
-        op("S", lambda: Sc.activation(out, a, f, **kw), reads, writes)
+    def act(out, a, f, reads, writes, n=None, per=1.0, **kw):
+        op("S", lambda: Sc.activation(out, a, f, **kw), reads, writes, n, per)
 
-    def mm(out, l, r, st, sp, reads, bank, inc=None):
-        op("P", lambda: P.matmul(out, l, r, st, sp), reads, [bank], sp if inc is None else inc)
+    def lin(out, a, scale, bias, reads, writes, n=None, per=1.0, e="VS"):
+        def fn(x=e):
+            if x == "S":
+                return Sc.activation(out, a, F.Identity, scale=scale, bias=bias)
+            return V.tensor_scalar(out, a, scale, bias, A.mult, A.add)
+        op(e, fn, reads, writes, n, per)
 
-    def iota(out, pat, base, chm, key, flt=True):
+    def iota(out, pat, base, chm, key, n, flt=True):
         if flt:
-            op("G", lambda: g.iota(out, pat, base, chm, allow_small_or_imprecise_dtypes=True), [], [key])
+            op("G", lambda: g.iota(out, pat, base, chm, allow_small_or_imprecise_dtypes=True), [], [key], n, 2)
         else:
-            op("G", lambda: g.iota(out, pat, base, chm), [], [key])
+            op("G", lambda: g.iota(out, pat, base, chm), [], [key], n, 2)
 
     PB = [T["p%d" % b] for b in range(8)]
     mine = slice(16 * me, 16 * me + 16)
-    pp, pm, pd = T.pf[:, 0:1], T.pf[:, 1:2], T.pf[:, 2:3]
+    col = lambda j: T.pf[:, j:j + 1]
+    pp, pm, pd = col(0), col(1), col(2)
     IB = T.shw[:, 128:256]
+    SZ = T.szb[:, 16:16 + S]
+    JT = ["jt%d" % j for j in range(9)]
+    TAB = ["tab%d" % j for j in range(9)]
+    GV = ["gv%d" % i for i in range(N)]
 
-    dma("Y", "drf", T.rfo[:], T.rf[:], [], ["rfo"])
-    dma("S", "ds1", T.s1[:, 0:112, :], T.sz[:], [], ["s1"])
-    dma("Y", "ds1", T.s1[:, 112:119, :], T.cd[:], [], ["s1"])
-    dma("S", "ds1", T.s1[:, 119:123, :], T.rch[:], [], ["s1"])
-    dma("Y", "ds1", T.s1[:, 123:128, :], T.sz[0:8, 0:320], [], ["s1"])
-    dma("Y", "dsz", T.szo[:], T.sz[:], [], ["szo"])
-    dma("Y", "dr1", T.r1[me, 0:112, :], T.sz[mine, :], [], ["r1"])
-    dma("Y", "dr1", T.r1[me, 112:119, :], T.cd[mine, :], [], ["r1"])
-    dma("Y", "dr1", T.r1[me, 119:123, :], T.rch[mine, :], [], ["r1"])
-    iota(T.pi[:, 0:1], [[0, 1]], 0, 1, "pi", False)
-    iota(T.ja[:], [[16, 28]], 0, 0, "ja")
-    iota(T.ion[:], [[1, S]], 0, 0, "ion")
-    iota(T.rv[:], [[0, 8], [1, 8]], 0, 0, "rv")
-    bulk_send(1)
-    iota(T.cm[:], [[0, 8], [1, 16]], 0, 0, "cm")
-    iota(T.cdv[:], [[1, 8], [0, 16]], 0, 0, "cdv")
-    iota(T.thr[:], [[0, 16], [16, 28]], W, 0, "thr")
+    dma("Y", "ds0", T.s0[:, 0:56, :], T.cd[:], [], ["s0"], 1.3, True)
+    dma("S", "ds0", T.s0[:, 56:88, :], T.rch[:], [], ["s0"], 1.3, True)
+    dma("S", "ds0", T.s0[:, 88:128, :], T.sz[0:8, 0:320], [], ["s0"], 1.3, True)
+    dma("Y", "dsz", T.szo[:], T.sz[:], [], ["szo"], 2.2, True)
+    dma("S", "drf", T.rfo[:], T.rf[:], [], ["rfo"], 3.0, True)
+    dma("Y", "dr0", T.r0[me, 0:56, :], T.cd[mine, :], [], ["r0"], 3.2, True)
+    dma("Y", "dr0", T.r0[me, 56:88, :], T.rch[mine, :], [], ["r0"], 3.2, True)
+    dma("Y", "dcd", T.cdo[:], T.cd[:], [], ["cdo"], 3.3, True)
+    iota(T.pi[:, 0:1], [[0, 1]], 0, 1, "pi", 1, False)
+    iota(T.ion[:], [[1, S]], 0, 0, "ion", S)
+    iota(T.rv[:], [[0, 8], [1, 8]], 0, 0, "rv", 64)
+    iota(T.cdv[:], [[1, 8], [0, 16]], 0, 0, "cdv", 128)
+    iota(T.cm[:], [[0, 8], [1, 16]], 0, 0, "cm", 128)
+    iota(T.xf[:], [[1, 4], [8, 8]], 0, 0, "xf", 32)
+    iota(T.thr[:], [[0, 16], [16, 28]], int(W + C0), 0, "thr", S)
+    wide[0] = 16
     for i, d in enumerate(order):
         ms(T.gv[:, 8 * i:8 * i + 8], float(d), ["gv%d" % i])
-    GV = ["gv%d" % i for i in range(N)]
     ts(T.pi[:, 1:2], T.pi[:, 0:1], 15, None, A.bitwise_and, None, ["pi"], ["pi1"])
     ts(T.pi[:, 2:3], T.pi[:, 0:1], 4, None, A.arith_shift_right, None, ["pi"], ["pi2"])
-    ts(T.pi[:, 3:4], T.pi[:, 0:1], 16, None, A.bitwise_and, None, ["pi"], ["pi3"])
+    ts(T.pi[:, 3:4], T.pi[:, 0:1], 1, None, A.arith_shift_right, None, ["pi"], ["pi3"])
+    ts(T.pi[:, 6:7], T.pi[:, 0:1], 1, None, A.bitwise_and, None, ["pi"], ["pi6"])
     cp(T.pf[:, 0:4], T.pi[:, 0:4], ["pi", "pi1", "pi2", "pi3"], ["pf"])
-    act(PB[1][:, 0:S], T.ion[:], F.Identity, ["ion"], ["p1"], bias=float(S * me))
-    ts(T.ja[:], T.ja[:], pm, None, A.add, None, ["ja", "pf"], ["ja"])
-    ts(T.jb[:], T.ja[:], -13.5, 1.0 / 28, A.add, A.mult, ["ja"], ["jb"])
-    cp(T.ji[:], T.jb[:], ["jb"], ["ji"])
-    cp(T.jb[:], T.ji[:], ["ji"], ["jb"])
-    ts(T.jc[:], T.jb[:], -28.0, None, A.mult, None, ["jb"], ["jc"])
-    tt(T.ji[:], T.jc[:], T.ja[:], A.add, ["jc", "ja"], ["ji"])
-    ts(T.jk[:], T.ji[:], 1, None, A.bitwise_and, None, ["ji"], ["jk"])
-    ts(T.jc[:], T.jk[:], 16.0, T.pf[:, 3:4], A.mult, A.not_equal, ["jk", "pf"], ["jc"])
-    tt(T.ja[:], T.ji[:], T.jk[:], A.subtract, ["ji", "jk"], ["ja"])
-    ts(T.ja[:], T.ja[:], 16.0, T.pf[:, 3:4], A.mult, A.add, ["ja", "pf"], ["ja"])
-    ts(T.jc[:], T.jc[:], float(S), None, A.mult, None, ["jc"], ["jc"])
-    tt(T.ja[:], T.ja[:], T.jb[:], A.add, ["ja", "jb"], ["ja"])
-    tt(T.ja[:], T.ja[:], T.jc[:], A.add, ["ja", "jc"], ["ja"])
-    cp(T.pl[:], T.ja[:], ["ja"], ["pl"])
-    ts(T.pf[:, 4:5], T.pf[:, 3:4], -2.0, 16.0, A.mult, A.add, ["pf"], ["pf4"])
-    ts(T.pf[:, 4:5], T.pf[:, 4:5], pp, None, A.add, None, ["pf", "pf4"], ["pf4"])
-    ts(T.swp[:], T.ion[:, 0:128], T.pf[:, 4:5], None, A.is_equal, None, ["ion", "pf4"], ["swp"])
-    ts(T.u16[:], T.ion[:, 0:16], pd, 8.0, A.add, A.is_ge, ["ion", "pf"], ["u16"])
-    ts(T.cv[:], T.u16[:], -8.0, None, A.mult, None, ["u16"], ["cv"])
-    tt(T.cv[:], T.cv[:], T.ion[:, 0:16], A.add, ["cv", "ion"], ["cv"])
-    ts(T.cv[:], T.cv[:], 2.0, 17.0, A.mult, A.add, ["cv"], ["cv"])
-    ts(T.t16[:, 8:9], pm, 1.0, None, A.is_equal, None, ["pf"], ["t16b"])
-    ts(T.cv[:], T.cv[:], T.t16[:, 8:9], None, A.mult, None, ["cv", "t16b"], ["cv"])
-    for j in range(6):
-        act(T.jt[:, S * j:S * j + S], T.ion[:], F.Identity, ["ion", "cv"], ["jt%d" % j], scale=0.0, bias=T.cv[:, j:j + 1])
-    tt(T.ta[:], T.rfo[:], PB[1][:, 0:S], A.is_ge, ["rfo", "p1"], ["ta"])
-    ts(PB[2][:, 0:S], T.ta[:], float(-W), float(W - S * me), A.mult, A.add, ["ta"], ["p2"])
-    tt(T.lo[:], T.rfo[:], PB[2][:, 0:S], A.add, ["rfo", "p2"], ["lo"])
-    op("V", lambda: V.transpose(T.yw[:, 0:S], T.lo[:]), ["lo"], ["yw0"])
-    mm(PB[0][:, 0:S], T.swp[:], T.yw[:, 0:S], True, True, ["swp", "yw0"], "p0")
-    act(T.yw[:, S:2 * S], PB[0][:, 0:S], F.Identity, ["p0"], ["yw1"])
-    ts(T.m2[:, S:2 * S], T.rfo[:], float(W - S * me), None, A.add, None, ["rfo"], ["m2b"])
-    cp(T.szob[:], T.szo[:], ["szo"], ["szob"])
-    act(T.to[:], T.szob[:], F.Identity, ["szob"], ["to", "tot0"], accum_out=T.tot[:, 0:1])
-    ts(T.mo[:], T.rv[:], float(me), None, A.is_gt, None, ["rv"], ["mo"])
-    ts(T.t64[:], T.gv[:], pd, None, A.is_gt, None, GV + ["pf"], ["t64"])
-    ts(T.u64[:], T.rv[:], float(me), None, A.is_equal, None, ["rv"], ["u64"])
-    tt(T.t64[:], T.t64[:], T.u64[:], A.mult, ["t64", "u64"], ["t64"])
-    tt(T.mo[:], T.mo[:], T.t64[:], A.add, ["mo", "t64"], ["mo"])
-    sums_send(0, T.mo, "mo")
-    cp(T.m2[:, 0:S], T.yw[:, 0:2 * S].indirect(T.pl[:, 0:28]), ["yw0", "yw1", "pl"], ["m2a"])
-    dma("Y", "ds2", T.s2[:, 64:128, :], T.m2[:, S:2 * S], ["m2b"], ["s2"])
-    dma("Y", "ds2", T.r2[me, 64:128, :], T.m2[mine, S:2 * S], ["m2b"], ["r2"])
-    dma("S", "ds2", T.s2[:, 0:64, :], T.m2[:, 0:S], ["m2a"], ["s2"])
-    dma("S", "ds2", T.r2[me, 0:64, :], T.m2[mine, 0:S], ["m2a"], ["r2"])
-    bulk_send(2)
-    dma("Y", "ds3", T.s3[:, 119:128, :], T.ion[0:72, 0:64], ["ion"], ["s3"])
-    dma("Y", "dw1", T.szi[:], T.r1[:, 0:112, :], ["r1"], ["szi"])
-    dma("Y", "dw1b", T.rci[:], T.r1[:, 119:123, :], ["r1"], ["rci"])
-    dma("Y", "dw1b", T.cdi[:], T.r1[:, 112:119, :], ["r1"], ["cdi"])
-    dma("Y", "dw2", T.lt[:], T.r2[:, 0:64, :], ["r2"], ["lt"])
-    dma("Y", "dw2b", T.ynu[:], T.r2[:, 64:128, :], ["r2"], ["ynu"])
-    ms(T.ones[:], 1.0, ["ones"])
-    ms(T.loc[:, 0:1], -CEN, ["loc0"])
-    ts(T.shw[:, 0:128], T.ion[:, 0:128], pp, -1.0, A.is_equal, A.mult, ["ion", "pf"], ["shw0"])
-    ts(T.shw[:, 128:256], T.ion[:, 0:128], pp, None, A.is_equal, None, ["ion", "pf"], ["shw"])
-    ts(T.idf[:], T.ion[:, 0:128], pp, None, A.is_equal, None, ["ion", "pf"], ["idf"])
-    ts(T.em[:], T.cm[:], pm, None, A.is_equal, None, ["cm", "pf"], ["em"])
-    ts(T.ct[:], T.ion[:, 0:8], pd, CNEG, A.is_lt, A.mult, ["ion", "pf"], ["ct"])
-    ts(T.t16[:, 0:8], T.ion[:, 0:8], pd, CPOS, A.is_gt, A.mult, ["ion", "pf"], ["t16"])
-    ts(T.ct[:], T.ct[:], -MID, None, A.add, None, ["ct"], ["ct"])
-    tt(T.ct[:], T.ct[:], T.t16[:, 0:8], A.add, ["ct", "t16"], ["ct"])
-    for j in range(6, 9):
-        act(T.jt[:, S * j:S * j + S], T.ion[:], F.Identity, ["ion", "cv"], ["jt%d" % j], scale=0.0, bias=T.cv[:, j:j + 1])
-    ts(T.sg[:], T.u16[:], 2.0, -1.0, A.mult, A.add, ["u16"], ["sg"])
+    cp(col(4), T.pi[:, 6:7], ["pi6"], ["pf4"])
     tt(T.pi[:, 4:5], T.pi[:, 1:2], T.pi[:, 2:3], A.add, ["pi1", "pi2"], ["pi4"])
     ts(T.pi[:, 5:6], T.pi[:, 4:5], 7, None, A.bitwise_and, None, ["pi4"], ["pi5"])
     cp(T.rot[:, 0:1], T.pi[:, 5:6], ["pi5"], ["rot"])
-    act(T.ibig[:], IB, F.Identity, ["shw"], ["ibig"], scale=-BIG)
-    act(T.i16[:], IB, F.Identity, ["shw"], ["i16"], scale=-16.0)
-    act(T.i32[:], IB, F.Identity, ["shw"], ["i32"], scale=32.0)
-    act(T.i1k[:], IB, F.Identity, ["shw"], ["i1k"], scale=1024.0)
-    act(T.onesb[:], T.ones[:], F.Identity, ["ones"], ["onesb"])
-    act(T.i38[:], IB, F.Identity, ["shw"], ["i38"], scale=W + 224.0)
-    act(T.nc[:], T.ion[:], F.Identity, ["ion"], ["nc"], bias=-224.0)
-    act(T.ncb[:], T.ion[:], F.Identity, ["ion"], ["ncb"], bias=-224.0)
-    ms(T.kv[:], BIG + K + CEN, ["kv"])
-    ts(T.pf[:, 5:6], pd, 16.0, 15.0, A.mult, A.add, ["pf"], ["pf5"])
-    ts(T.uw[:], T.ion[:, 0:144], T.pf[:, 5:6], None, A.is_equal, None, ["ion", "pf5"], ["uw"])
+    cp(T.xl[:], T.xf[:], ["xf"], ["xl"])
+    ms(T.szb[:, 0:16], 0.0, ["sz0"])
+    ms(T.ln[:, 0:8], 0.0, ["ln0"])
+    ts(col(5), pm, 1.0, None, A.is_equal, None, ["pf"], ["pf5"])
+    ts(col(7), pm, 0.0, None, A.is_equal, None, ["pf"], ["pf7"])
+    ts(col(11), pm, float(NA), None, A.is_ge, None, ["pf"], ["pf11"])
+    ts(col(19), pd, float(me), None, A.is_lt, None, ["pf"], ["pf19"])
+    ts(col(20), pd, float(me), None, A.is_equal, None, ["pf"], ["pf20"])
+    for j, src, sk, a, b in ((6, pd, "pf", 16.0, 15.0), (8, col(5), "pf5", float(S), col(7)), (9, col(3), "pf", 16.0, 15.0),
+                             (10, col(4), "pf4", S - 1.0, 1.0), (12, col(11), "pf11", 2 * BIG, -BIG), (21, col(11), "pf11", -2 * BIG, BIG),
+                             (13, col(11), "pf11", -S * MAG - 0.5, 0.5), (14, col(11), "pf11", -1000.0, 0.0), (15, col(11), "pf11", float(-S), 0.0),
+                             (16, col(11), "pf11", -1.0, 0.0), (17, pd, "pf", float(S), -C0 - W), (18, pd, "pf", float(S), 224.0)):
+        lin(col(j), src, a, b, [sk, "pf7"], ["pf%d" % j])
+    ts(T.u16[:], T.ion[:, 0:16], pd, 8.0, A.add, A.is_ge, ["ion", "pf"], ["u16"])
+    lin(T.cv[:], T.u16[:], -8.0, MAG, ["u16"], ["cv"])
+    tt(T.cv[:], T.cv[:], T.ion[:, 0:16], A.add, ["cv", "ion"], ["cv"])
+    lin(T.cv[:], T.cv[:], col(5), 0.0, ["cv", "pf5"], ["cv"])
+    lin(T.sg[:], T.u16[:], 2.0, -1.0, ["u16"], ["sg"])
+    ts(T.ct[:], T.ion[:, 0:8], pd, CNEG, A.is_lt, A.mult, ["ion", "pf"], ["ct"])
+    ts(T.t16[:, 0:8], T.ion[:, 0:8], pd, CPOS, A.is_gt, A.mult, ["ion", "pf"], ["t16"])
+    lin(T.ct[:], T.ct[:], 1.0, -MID, ["ct"], ["ct"])
+    tt(T.ct[:], T.ct[:], T.t16[:, 0:8], A.add, ["ct", "t16"], ["ct"])
+    ts(T.d20[:], T.gv[:, 0:64:8], pd, 20.0, A.is_equal, A.mult, GV + ["pf"], ["d20"])
+    lin(T.d64[:], T.d20[:], 3.2, 0.0, ["d20"], ["d64"])
+    lin(T.d65[:], T.d20[:], -3.2, 0.0, ["d20"], ["d65"])
+    lin(T.mk[:, 0:8], T.ion[:, 0:8], 0.0, 1.0, ["ion"], ["mk0"])
+    ts(T.mk[:, 8:16], T.ion[:, 0:8], pd, None, A.is_lt, None, ["ion", "pf"], ["mk"])
+    wide[0] = 64
+    ms(T.xs[:, 64 * RO:64 * RO + 64], 0.0, ["xz"])
+    for m, mk, a, b in ((T.mo, "mo", float(me), pd), (T.mw, "mw", pd, float(me))):
+        ts(m[:], T.rv[:], a, None, A.is_gt, None, ["rv", "pf"], [mk])
+        ts(T.t64[:], T.gv[:], b, None, A.is_gt, None, GV + ["pf"], ["t64"])
+        ts(T.u64[:], T.rv[:], a, None, A.is_equal, None, ["rv", "pf"], ["u64"])
+        tt(T.t64[:], T.t64[:], T.u64[:], A.mult, ["t64", "u64"], ["t64"], per=2)
+        tt(m[:], m[:], T.t64[:], A.add, [mk, "t64"], [mk], per=2)
+    wide[0] = 128
+    ts(T.shw[:, 128:256], T.ion[:, 0:128], pp, None, A.is_equal, None, ["ion", "pf"], ["shw"])
+    ts(T.em[:], T.cm[:], pm, None, A.is_equal, None, ["cm", "pf"], ["em"])
+    ts(T.b512[:], T.cdv[:], pd, 512.0, A.is_equal, A.mult, ["cdv", "pf"], ["b512"])
+    ts(T.rep[:], T.cdv[:], pp, 1024.0, A.is_equal, A.mult, ["cdv", "pf"], ["rep"])
+    ts(T.uw[:], T.ion[:, 0:144], col(6), None, A.is_equal, None, ["ion", "pf6"], ["uw"])
+    ts(T.w1[:], T.ion[:, 0:144], col(9), col(10), A.is_equal, A.mult, ["ion", "pf9", "pf10"], ["w1"])
+    lin(T.ww[:], T.uw[:], col(8), 0.0, ["uw", "pf8"], ["ww"])
+    lin(T.b20[:], T.b512[:], 20.0 / 512, 0.0, ["b512"], ["b20"])
+    lin(T.kv[:], IB, 0.0, K + CEN, ["shw"], ["kv"])
+    for out, key, sc, sk in ((T.shw[:, 0:128], "shw0", -1.0, "shw"), (T.idf[:], "idf", 1.0, "shw"), (T.iw[:], "iw", float(-W), "shw"), (T.ip[:], "ip", BIG, "shw"),
+                             (T.im[:], "im", -BIG, "shw"), (T.i16[:], "i16", -16.0, "shw"), (T.i32[:], "i32", 32.0, "shw"), (T.i448[:], "i448", float(S), "shw"),
+                             (T.na[:], "na", col(11), "pf11"), (T.nb[:], "nb", col(15), "pf15"), (T.nd[:], "nd", col(16), "pf16"),
+                             (T.ne[:], "ne", col(12), "pf12"), (T.nf[:], "nf", col(21), "pf21")):
+        lin(out, IB, sc, 0.0, ["shw", sk], [key])
+    lin(T.ema[:], T.em[:], col(19), 0.0, ["em", "pf19"], ["ema"])
+    lin(T.emb[:], T.em[:], col(20), 0.0, ["em", "pf20"], ["emb"])
+    wide[0] = S
+    lin(T.ones[:], T.ion[:], 0.0, 1.0, ["ion"], ["ones"])
+    lin(T.onesb[:], T.ion[:], 0.0, 1.0, ["ion"], ["onesb"])
+    lin(T.nc[:], T.ion[:], 1.0, -224.0, ["ion"], ["nc"])
+    lin(T.ncb[:], T.ion[:], 1.0, -224.0, ["ion"], ["ncb"])
+    lin(T.thr[:], T.thr[:], 1.0, pm, ["thr", "pf"], ["thr"])
+    if NA:
+        lin(T.nlc[:, 0:28 * NA], T.thr[:, 0:28 * NA], 1.0, -(W + C0 + 224.0), ["thr"], ["nlc"], 28 * NA)
+    for j in range(9):
+        lin(T.jt[:, S * j:S * j + S], T.ion[:], 0.0, T.cv[:, j:j + 1], ["ion", "cv"], ["jt%d" % j])
+    bulk_send(0)
+    cp(T.szob[:], T.szo[:], ["szo"], ["szob"])
+    dma("Y", "ds1", T.s1[:], T.szob[:], ["szob"], ["s1"])
+    dma("Y", "ds1", T.r1[me], T.szob[mine, :], ["szob"], ["r1"])
+    bulk_send(1)
+    ts(T.m2[:, S:2 * S], T.rfo[:], 1.0 / S, MAG - me - 223.5 / S, A.mult, A.add, ["rfo"], ["m2b"])
+    ts(PB[2][:, 0:S], T.m2[:, S:2 * S], float(-S), S * (MAG - me) - 224.0, A.mult, A.add, ["m2b"], ["p2"])
+    tt(T.m2[:, 0:S], T.rfo[:], PB[2][:, 0:S], A.add, ["rfo", "p2"], ["m2a"])
+    dma("Y", "ds2", T.s2[:, 64:128, :], T.m2[:, S:2 * S], ["m2b"], ["s2"])
+    dma("Y", "ds2", T.r2[me, 64:128, :], T.m2[mine, S:2 * S], ["m2b"], ["r2"])
+    dma("Y", "ds2", T.s2[:, 0:64, :], T.m2[:, 0:S], ["m2a"], ["s2"])
+    dma("Y", "ds2", T.r2[me, 0:64, :], T.m2[mine, 0:S], ["m2a"], ["r2"])
+    bulk_send(2)
+    act(T.to[:], T.szob[:], F.Identity, ["szob"], ["to", "tot0"], accum_out=T.tot[:, 0:1])
+    sums_send(0, T.mo, "mo")
+    cp(T.cdm[:], T.cdo[:], ["cdo"], ["cdm"], 28)
+    lin(T.cbo[:], T.nc[:, 0:S].indirect(T.cdm[:, 0:28]), 1.0, 0.0, ["nc", "cdm"], ["cbo"], per=GAT)
+    lin(T.m6[:, S:2 * S], T.m2[:, S:2 * S], 1.0, 0.0, ["m2b"], ["m6b"], e="S")
+    lin(T.m6[:, 0:S], T.m2[:, 0:S], 1.0, 0.0, ["m2a"], ["m6a"], e="S")
+    tt(T.sm[:], T.m2[:, S:2 * S].indirect(T.cdm[:, 0:28]), T.m6[:, S:2 * S], A.not_equal, ["m2b", "m6b", "cdm"], ["sm"], per=GAT)
+    tt(T.mis[:], T.m2[:, 0:S].indirect(T.cdm[:, 0:28]), T.m6[:, 0:S], A.not_equal, ["m2a", "m6a", "cdm"], ["mis"], per=GAT)
+    mms([(PB[3][:, 0:S], IB, T.cbo[:], True, False, ["shw", "cbo"], S), (PB[3][:, 0:S], T.b512[:], T.sm[:], False, True, ["b512", "sm"], S)], "p3")
+    mms([(PB[4][:, 0:S], IB, T.cbo[:], True, False, ["shw", "cbo"], S), (PB[4][:, 0:S], T.b512[:], T.sm[:], False, False, ["b512", "sm"], S),
+         (PB[4][:, 0:S], T.b512[:], T.mis[:], False, True, ["b512", "mis"], S)], "p4")
+    ts(T.m5[:, S:2 * S], PB[3][:, 0:S], 224.0, None, A.min, None, ["p3"], ["m5b"])
+    tt(T.m5[:, 0:S], PB[4][:, 0:S], T.nc[:], A.min, ["p4", "nc"], ["m5a"])
+    dma("Y", "ds5", T.s5[:, 64:128, :], T.m5[:, S:2 * S], ["m5b"], ["s5"])
+    dma("Y", "ds5", T.r5[me, 64:128, :], T.m5[mine, S:2 * S], ["m5b"], ["r5"])
+    dma("Y", "ds5", T.s5[:, 0:64, :], T.m5[:, 0:S], ["m5a"], ["s5"])
+    dma("Y", "ds5", T.r5[me, 0:64, :], T.m5[mine, 0:S], ["m5a"], ["r5"])
+    bulk_send(5)
+    dma("Y", "ds3", T.s3[:, 119:128, :], T.ion[0:72, 0:64], ["ion"], ["s3"])
+    dma("Y", "dw1b", T.rci[:], T.r0[:, 56:88, :], ["r0"], ["rci"])
+    dma("Y", "dw1b", T.cdi[:], T.r0[:, 0:56, :], ["r0"], ["cdi"])
+    dma("Y", "dw1", SZ, T.r1[:], ["r1", "sz0"], ["szb"])
+    dma("Y", "dw2", T.g1[0:16, :], T.r2[:], ["r2"], ["g1"])
+    dma("Y", "dw2b", T.ref[:], T.r2[:, 0:64, :], ["r2"], ["ref"])
+    dma("Y", "dw2b", T.sl[:], T.r2[:, 64:128, :], ["r2"], ["sl"])
+    dma("Y", "dw5", T.jv[:, S:2 * S], T.r5[:, 0:64, :], ["r5"], ["jv1"])
+    dma("Y", "dw5", T.cb[:], T.r5[:, 64:128, :], ["r5"], ["cb"])
+    cp(T.cdl[:], T.cdi[:], ["cdi"], ["cdl"], 28)
+    if NA:
+        ts(T.bk[:, 0:NA], T.rci[:, 0:NA], -1.0, None, A.mult, None, ["rci"], ["bka"], 16)
+    ts(T.bk[:, NA:16], T.rci[:, NA:16], -0.5 * K, None, A.add, None, ["rci", "bka"], ["bk"], 16)
 
-    def late_constants():
-        ts(T.pf[:, 6:7], pm, 0.0, None, A.is_equal, None, ["pf"], ["pf6"])
-        ts(T.pf[:, 7:8], pm, 1.0, None, A.is_equal, None, ["pf"], ["pf7"])
-        ts(T.pf[:, 8:9], T.pf[:, 7:8], 224.0, T.pf[:, 6:7], A.mult, A.add, ["pf6", "pf7"], ["pf8"])
-        ts(T.ww[:], T.uw[:], T.pf[:, 8:9], None, A.mult, None, ["uw", "pf8"], ["ww"])
-        ts(T.b20[:], T.cdv[:], pd, 20.0, A.is_equal, A.mult, ["cdv", "pf"], ["b20"])
-        ts(T.b512[:], T.cdv[:], pd, 512.0, A.is_equal, A.mult, ["cdv", "pf"], ["b512"])
-        ts(T.rep[:], T.cdv[:], pp, 1024.0, A.is_equal, A.mult, ["cdv", "pf"], ["rep"])
-        ts(T.mw[:], T.rv[:], pd, None, A.is_gt, None, ["rv", "pf"], ["mw"])
-        ts(T.t64[:], T.gv[:], float(me), None, A.is_gt, None, GV, ["t64"])
-        ts(T.u64[:], T.rv[:], pd, None, A.is_equal, None, ["rv", "pf"], ["u64"])
-        tt(T.t64[:], T.t64[:], T.u64[:], A.mult, ["t64", "u64"], ["t64"])
-        tt(T.mw[:], T.mw[:], T.t64[:], A.add, ["mw", "t64"], ["mw"])
-        ts(T.mf[:], T.gv[:], pd, None, A.is_gt, None, GV + ["pf"], ["mf"])
-        ts(T.mf[:, 1:64:8], T.gv[:, 1:64:8], pd, None, A.is_equal, None, GV + ["pf", "mf"], ["mf"])
-        act(T.ez[:, 0:128], T.em[:], F.Identity, ["em"], ["ez0"], scale=0.0)
-        act(T.ez[:, 128:256], T.em[:], F.Identity, ["em"], ["ez"])
-        ts(T.pf[:, 9:10], pd, float(S), float(-W), A.mult, A.add, ["pf"], ["pf9"])
-        ts(T.pf[:, 10:11], pd, float(S), 224.0, A.mult, A.add, ["pf"], ["pf10"])
+    def JV(t):
+        return T.jv[:, S * (t % 2):S * (t % 2) + S]
 
-    act(T.thr[:], T.thr[:], F.Identity, ["thr", "pf"], ["thr"], bias=pm)
-    late_constants()
-    JT = ["jt%d" % j for j in range(9)]
-    TAB = ["tab%d" % j for j in range(9)]
+    def keys(name, a, b):
+        return [name + str(k) for k in range(a, b)]
 
-    def base_near(b):
-        mm(PB[b][:, S:S + 8], T.idf[:], T.ct[:], True, False, ["idf", "ct"], "p%d" % b)
+    def rename(k):
+        lin(T.gr[:, S * k:S * k + S], T.jt[:, 0:9 * S].indirect(T.lt[:, 28 * k:28 * k + 28]), 1.0, 0.0, JT + ["lt%d" % k], ["gr%d" % k], per=GAT)
 
-    def base_far(t, b):
-        o = 64 * t
-        tt(T.t64[:, 0:32], T.xr[:, o:o + 32], T.xr[:, o + 32:o + 64], A.add, ["xr%d" % t, "xo%d" % t], ["t64"])
-        tt(T.u64[:, 0:16], T.t64[:, 0:16], T.t64[:, 16:32], A.add, ["t64"], ["u64"])
-        tt(T.t64[:, 0:8], T.u64[:, 0:8], T.u64[:, 8:16], A.add, ["u64"], ["t64"])
-        mm(PB[b][:, S:S + 8], T.em[:], T.t64[:, 0:8], False, True, ["em", "t64"], "p%d" % b)
-
-    def rename(e, a, b):
-        src = T.jt[:, 0:9 * S].indirect(T.lt[:, 32 * a:32 * b])
-        out = T.gr[:, 512 * a:512 * b]
-        keys = ["gr%d" % u for u in range(a, b)]
-        if e == "V":
-            cp(out, src, JT + ["lt"], keys)
+    def listed(t, a, b):
+        c, n = slice(28 * a, 28 * b), 28 * (b - a)
+        if t:
+            mms([(PB[0][:, c], T.ww[:, 15 - q:143 - q], T.gr[:, S * a + q:S * b:16], q == 0, q == 15, ["ww"] + keys("gr", a, b), n) for q in range(16)], "p0")
         else:
-            act(out, src, F.Identity, JT + ["lt"], keys)
+            mms([(PB[0][:, c], T.w1[0:16, 15 - q:143 - q], T.g1[0:16, S * a + q:S * b:16], q == 0, q == 15,
+                  ["w1", "g1"] + (["tab%d" % BB] if a else []), n) for q in range(16)], "p0")
+        tt(T.ta[:, c], PB[0][:, c], T.thr[:, c], A.is_ge, ["p0", "thr"], keys("ta", a, b), n)
+        ts(T.tb[:, c], T.ta[:, c], float(-W), None, A.mult, None, keys("ta", a, b), keys("tb", a, b), n, 0.5)
+        tt(T.tc[:, c], PB[0][:, c], T.tb[:, c], A.add, ["p0"] + keys("tb", a, b), keys("tc", a, b), n)
+        ts(T.lt[:, c], T.tc[:, c], -C0, None, A.add, None, keys("tc", a, b), keys("lt", a, b), n)
 
-    def turn(a, b):
-        for q in range(16):
-            mm(PB[0][:, 32 * a:32 * b], T.ww[:, 15 - q:143 - q], T.gr[:, 512 * a + q:512 * b:16], q == 0, q == 15,
-               ["ww"] + ["gr%d" % u for u in range(a, b)], "p0", q == 15)
+    def slot(j):
+        l = T.shw[:, 16 * j:16 * j + 128]
+        mms([(PB[j][:, 0:S], l, T.hi[:], True, False, ["shw", "shw0", "hi"], S)], "p%d" % j)
+        mms([(PB[j][:, 0:S], l, T.lw[:], False, True, ["shw", "shw0", "lw"], S)], "p%d" % j)
 
-    def empty(e, j):
-        out = T.tab[:, S * j:S * j + S]
-        if e == "V":
-            ts(out, PB[j][:, 0:S], T.cs[:, j:j + 1], None, A.add, None, ["p%d" % j, "cs"], ["tab%d" % j])
-        else:
-            act(out, PB[j][:, 0:S], F.Identity, ["p%d" % j, "cs"], ["tab%d" % j], bias=T.cs[:, j:j + 1])
+    def limit(k):
+        lin(T.gg[:, S * k:S * k + S], T.tab[:, 0:9 * S].indirect(T.ol[:, 28 * k:28 * k + 28]), 1.0, T.bk[:, k:k + 1], TAB + ["ol", "bk"], ["gg%d" % k], per=GAT)
 
-    def lengths(t):
-        far = T.far[:, S * (t % 2):S * (t % 2) + S]
-        ts(far, PB[2][:, 0:S], 0.0, None, A.not_equal, None, ["p2"], ["far%d" % (t % 2)])
+    def table(t):
+        src, sk = (T.ln[:, 7:7 + S], ["ln", "ln0"]) if t else (T.szb[:, 15:15 + S], ["szb", "sz0"])
+        op("V", lambda: V.tensor_tensor_scan(PB[7][:, 0:S], T.ones[:], src, -CEN, A.mult, A.add), ["ones"] + sk, ["p7"])
+        cp(T.hi[:], PB[7][:, 0:S], ["p7"], ["hi"])
+        tt(T.lw[:], PB[7][:, 0:S], T.hi[:], A.subtract, ["p7", "hi"], ["lw"])
+        lin(T.tab[:, 0:S], PB[7][:, 0:S], -1.0, -CPOS, ["p7"], ["tab0"])
+        lin(T.tab[:, 8 * S:9 * S], PB[7][:, 0:S], 1.0, CNEG, ["p7"], ["tab8"])
+        if t:
+            for k in range(16):
+                rename(k)
+            dma("Y", "dn%d" % (t - 1), T.ref[:], T.gr[0:128:16, :], keys("gr", 0, 16), ["ref"])
+            dma("Y", "dn%d" % (t - 1), T.nth[:], T.gr[0:128:16, :], keys("gr", 0, 16), ["nth"], 2.3)
+        for a, b in (PARTS if t else PARTS0[:1]):
+            listed(t, a, b)
+        if NA:
+            mms([(PB[7][:, 0:28 * NA], IB, T.nlc[:, 0:28 * NA], True, False, ["shw", "nlc"], 28 * NA),
+                 (PB[7][:, 0:28 * NA], T.iw[:], T.ta[:, 0:28 * NA], False, True, ["iw"] + keys("ta", 0, NA), 28 * NA)], "p7")
+            ts(T.ol[:, 0:28 * NA], PB[7][:, 0:28 * NA], W + 224.0, None, A.add, None, ["p7"], ["ol"], 28 * NA)
+        for j in range(1, 8):
+            if j != BB:
+                slot(j)
+        if t:
+            for k in range(NA):
+                limit(k)
+        o, b = 64 * t, BB
+        tt(T.t64[:, 0:32], T.xr[:, o:o + 32], T.xr[:, o + 32:o + 64], A.add, ["xr%d" % t, "xo%d" % t], ["t64"], 64)
+        tt(T.u64[:, 0:16], T.t64[:, 0:16], T.t64[:, 16:32], A.add, ["t64"], ["u64"], 32)
+        tt(T.t64[:, 0:8], T.u64[:, 0:8], T.u64[:, 8:16], A.add, ["u64"], ["t64"], 16)
+        mms([(PB[b][:, S:S + 8], T.idf[:], T.ct[:], True, False, ["idf", "ct"], 256),
+             (PB[b][:, S:S + 8], T.em[:], T.t64[:, 0:8], False, True, ["em", "t64"], 256)], "p%d" % b)
+        cp(T.bs[:], PB[b][:, S:S + 8], ["p%d" % b], ["bs"], 16)
+        slot(b)
+        cp(T.ro[:], T.bs[:, 0:8].indirect(T.rot[:, 0:1]), ["bs", "rot"], ["ro"], 25)
+        ts(T.c1[:], T.ro[:], T.ro[:, 0:1], CPOS, A.subtract, A.max, ["ro"], ["c1"], 16)
+        tt(T.cs[:], T.c1[:], T.sg[:], A.mult, ["c1", "sg"], ["cs"], 32)
+        for j in range(1, 8):
+            lin(T.tab[:, S * j:S * j + S], PB[j][:, 0:S], 1.0, T.cs[:, j:j + 1], ["p%d" % j, "cs"], ["tab%d" % j])
+        if not t:
+            for k in range(NA):
+                limit(k)
+        dead = [(PB[1][:, 0:S], T.ip[:], T.ncb[:], True, False, ["ip", "ncb"], S), (PB[1][:, 0:S], T.im[:], JV(t), False, False, ["im", "jv%d" % (t % 2)], S)] if t else []
+        mms(dead + [(PB[1][:, 0:S], T.kv[0:1, :], T.onesb[0:1, :], not t, False, ["kv", "onesb"], S), (PB[1][:, 0:S], IB, T.hi[:], False, False, ["shw", "hi"], S),
+                    (PB[1][:, 0:S], IB, T.lw[:], False, True, ["shw", "lw"], S)], "p1")
+        for a, b in ([] if t else PARTS0[1:]):
+            listed(t, a, b)
+
+    def test(t):
+        jv, jk = JV(t), "jv%d" % (t % 2)
+        total = 17 + (t > 1)
+        done = [0]
+
+        def flags():
+            done[0] += 1
+            return done[0] == 1, done[0] == total
+
+        def count(l, r, reads):
+            mms([(PB[2][:, 0:S], l, r, None, None, reads, S)], "p2", flags)
+
+        if t > 1:
+            tt(T.mis[:], T.ref[:, 0:S].indirect(T.cdl[:, 0:28]), T.nth[:], A.not_equal, ["ref", "nth", "cdl"], ["mis"], per=GAT)
+            mms([(PB[4][:, 0:S], IB, T.cb[:], True, False, ["shw", "cb"], S), (PB[4][:, 0:S], T.b512[:], T.mis[:], False, True, ["b512", "mis"], S)], "p4")
+            tt(jv, PB[4][:, 0:S], T.nc[:], A.min, ["p4", "nc"], [jk])
+        o = S * (t % 2)
+        if t < RO:
+            for j in range(9):
+                a = j % 8
+                dma("Y", "dj%d" % (t - 1), T.jt[0:128 - 16 * a:16, S * j:S * j + S], T.jv[16 * a:128:16, o:o + S], [jk], ["jt%d" % j], 1.3)
+                if a:
+                    dma("Y", "dj%d" % (t - 1), T.jt[128 - 16 * a:128:16, S * j:S * j + S], T.jv[0:16 * a:16, o:o + S], [jk], ["jt%d" % j], 1.3)
+        dead = [(PB[6][:, 0:S], T.ne[:], JV(t - 1), True, False, ["ne", "jv%d" % ((t - 1) % 2)], S), (PB[6][:, 0:S], T.nf[:], T.ncb[:], False, False, ["nf", "ncb"], S)] if t > 1 else []
+        mms(dead + [(PB[6][:, 0:S], T.na[:], T.ncb[:], t == 1, False, ["na", "ncb"], S), (PB[6][:, 0:S], T.nb[:], T.sl[:], False, False, ["nb", "sl"], S),
+                    (PB[6][:, 0:S], T.nd[:], T.ref[:], False, True, ["nd", "ref"], S)], "p6")
+        ts(T.neg[:], PB[6][:, 0:S], col(13), None, A.is_gt, None, ["p6", "pf13"], ["neg"])
+        count(T.i16[:], T.neg[:], ["i16", "neg"])
+        if t > 1:
+            count(T.i32[:], T.far[:, S - o:2 * S - o], ["i32", "far%d" % ((t - 1) % 2)])
+        mms([(PB[5][:, 0:S], T.ip[:], jv, True, False, ["ip", jk], S), (PB[5][:, 0:S], T.im[:], T.ncb[:], False, False, ["im", "ncb"], S),
+             (PB[5][:, 0:S], IB, SZ, False, False, ["shw", "szb"], S)], "p5")
         if t == RO:
-            dma("Y", "ds4", T.s4[:], far, ["far0"], ["s4"])
-            dma("Y", "ds4", T.r4[me], T.far[mine, 0:S], ["far0"], ["r4"])
-        mm(PB[5][:, 0:S], T.b20[:], far, False, True, ["b20", "far%d" % (t % 2)], "p5")
-        act(T.ln[:], PB[5][:, 0:S], F.Relu, ["p5"], ["ln", "tot%d" % t], bias=-1024.0, accum_out=T.tot[:, t:t + 1])
-
-    def gap(t):
-        ren = t > 0
-        if ren:
-            rename("S", 1, 3)
-            lengths(t)
-            sums_send(t, T.mw, "mw")
-            rename("V", 0, 1)
-            turn(0, 3)
-            rename("S", 3, 6)
-            src, sk = T.ln, "ln"
-        else:
-            cp(T.szb[:], T.szi[:], ["szi"], ["szb"])
-            src, sk = T.szb, "szb"
-        op("V", lambda: V.tensor_tensor_scan(T.loc[:, 1:S], T.ones[:, 0:S - 1], src[:, 0:S - 1], -CEN, A.mult, A.add), ["ones", sk], ["loc"])
-        cp(T.hi[:], T.loc[:], ["loc", "loc0"], ["hi"])
-        tt(T.lw[:], T.loc[:], T.hi[:], A.subtract, ["loc", "loc0", "hi"], ["lw"])
-        def own():
-            act(T.tab[:, 0:S], T.loc[:], F.Identity, ["loc", "loc0"], ["tab0"], scale=-1.0, bias=-CPOS)
-            act(T.tab[:, 8 * S:9 * S], T.loc[:], F.Identity, ["loc", "loc0"], ["tab8"], bias=CNEG)
-
-        if not ren:
-            own()
-            ts(T.bk[:], T.rci[:], -0.5 * K, None, A.add, None, ["rci"], ["bk"])
-            base_near(0)
-        js = [7, 1, 5, 2, 6, 3, 4]
-        for j in js[:4]:
-            mm(PB[j][:, 0:S], T.shw[:, 16 * j:16 * j + 128], T.hi[:], True, False, ["shw", "shw0", "hi"], "p%d" % j)
-        if not ren:
-            base_far(t, 0)
-        for j in js:
-            if j not in js[:4]:
-                mm(PB[j][:, 0:S], T.shw[:, 16 * j:16 * j + 128], T.hi[:], True, False, ["shw", "shw0", "hi"], "p%d" % j)
-            mm(PB[j][:, 0:S], T.shw[:, 16 * j:16 * j + 128], T.lw[:], False, True, ["shw", "shw0", "lw"], "p%d" % j)
-        if ren:
-            rename("V", 6, 9)
-            rename("S", 9, 12)
-            rename("V", 12, 14)
-            own()
-            base_near(7)
-            turn(3, 6)
-            turn(6, 9)
-            turn(9, 12)
-            base_far(t, 7)
-            turn(12, 14)
-        bb = 7 if ren else 0
-        cp(T.bs[:], PB[bb][:, S:S + 8], ["p%d" % bb], ["bs"])
-        cp(T.ro[:], T.bs[:, 0:8].indirect(T.rot[:, 0:1]), ["bs", "rot"], ["ro"])
-        ts(T.c1[:], T.ro[:], T.ro[:, 0:1], CPOS, A.subtract, A.max, ["ro"], ["c1"])
-        tt(T.cs[:], T.c1[:], T.sg[:], A.mult, ["c1", "sg"], ["cs"])
-        al = T.al[:, S * (t % 2):S * (t % 2) + S] if ren else T.onesb[:]
-        ak = "al%d" % (t % 2) if ren else "onesb"
-        empty("V", 1)
-        empty("S", 7)
-        mm(PB[1][:, 0:S], T.kv[0:1, :], T.onesb[0:1, :], True, False, ["kv", "onesb"], "p1")
-        mm(PB[1][:, 0:S], T.ibig[:], al, False, False, ["ibig", ak], "p1")
-        mm(PB[1][:, 0:S], IB, T.hi[:], False, False, ["shw", "hi"], "p1")
-        mm(PB[1][:, 0:S], IB, T.lw[:], False, True, ["shw", "lw"], "p1")
-        if ren:
-            tt(T.ta[:], PB[0][:, 0:S], T.thr[:], A.is_ge, ["p0", "thr"], ["ta"])
-            ts(T.tb[:], T.ta[:], float(-W), None, A.mult, None, ["ta"], ["tb"])
-            tt(T.tc[:], PB[0][:, 0:S], T.tb[:], A.add, ["p0", "tb"], ["tc"])
-        empty("S" if ren else "V", 2)
-        empty("S", 5)
-        empty("S", 6)
-        empty("V", 3)
-        empty("S" if ren else "V", 4)
-        if ren:
-            cp(T.lt[:], T.tc[:], ["tc"], ["lt"])
-        else:
-            cp(T.cdl[:], T.cdi[:], ["cdi"], ["cdl"])
-            cp(T.cb[:], T.nc[:, 0:S].indirect(T.cdl[:, 0:28]), ["nc", "cdl"], ["cb"])
-
-    def main(t):
-        al = T.al[:, S * (t % 2):S * (t % 2) + S]
-        ak = "al%d" % (t % 2)
-        GR = ["gr%d" % c for c in range(14)]
-
-        def side0():
-            if t == 1:
-                cp(T.ref[:], T.ynu[:], ["ynu"], ["ref"])
-                cp(T.nth[:], T.ynu[:], ["ynu"], ["nth"])
-            else:
-                for k in range(16):
-                    mm(PB[3][:, 0:S], T.ww[:, 15 - k:143 - k], T.gr[:, S * k:S * k + S], k == 0, k == 15, ["ww"] + GR, "p3")
-
-        def side1():
-            if t > 1:
-                cp(T.ref[:], PB[3][:, 0:S], ["p3"], ["ref"])
-                cp(T.nth[:], PB[3][:, 0:S], ["p3"], ["nth"])
-            was = T.al[:, S * ((t - 1) % 2):S * ((t - 1) % 2) + S] if t > 1 else T.onesb[:]
-            mm(PB[6][:, 0:S], IB, T.ncb[:], True, False, ["shw", "ncb"], "p6")
-            mm(PB[6][:, 0:S], T.i38[:], was, False, True, ["i38", "al%d" % ((t - 1) % 2) if t > 1 else "onesb"], "p6")
-            mm(PB[4][:, 0:S], IB, T.cb[:], True, False, ["shw", "cb"], "p4")
-
-        def side2():
-            tt(T.mis[:], T.ref[:, 0:S].indirect(T.cdl[:, 0:28]), T.nth[:], A.not_equal, ["ref", "nth", "cdl"], ["mis"])
-            mm(PB[4][:, 0:S], T.b512[:], T.mis[:], False, True, ["b512", "mis"], "p4")
-
-        def side3():
-            tt(T.neg[:], T.ref[:], PB[6][:, 0:S], A.is_lt, ["ref", "p6"], ["neg"])
-            mm(PB[2][:, 0:S], T.i16[:], T.neg[:], False, False, ["i16", "neg"], "p2")
-
-        def side4():
-            if t < RO:
-                tt(T.jv[:], PB[4][:, 0:S], T.nc[:], A.min, ["p4", "nc"], ["jv"])
-                for j in range(9):
-                    a = j % 8
-                    dma("Y", "dj%d" % (t - 1), T.jt[0:128 - 16 * a:16, S * j:S * j + S], T.jv[16 * a:128:16, :], ["jv"], ["jt%d" % j])
-                    if a:
-                        dma("Y", "dj%d" % (t - 1), T.jt[128 - 16 * a:128:16, S * j:S * j + S], T.jv[0:16 * a:16, :], ["jv"], ["jt%d" % j])
-            else:
-                tt(T.tc[:], PB[4][:, 0:S], T.nc[:], A.min, ["p4", "nc"], ["tc"])
-                ts(T.yjf[:], T.tc[:], T.pf[:, 10:11], None, A.add, None, ["tc", "pf10"], ["yjf"])
-                ts(T.yrf[:], T.ref[:], T.pf[:, 9:10], None, A.add, None, ["ref", "pf9"], ["yrf"])
-                dma("Y", "ds3", T.s3[:, 0:112, :], T.yrf[:], ["yrf"], ["s3"])
-                dma("Y", "ds3", T.s3[:, 112:119, :], T.yjf[0:128:16, :], ["yjf"], ["s3"])
-                dma("Y", "ds3", T.r3[me, 0:112, :], T.yrf[mine, :], ["yrf"], ["r3"])
-                dma("Y", "ds3", T.r3[me, 112:119, :], T.yjf[16 * me:16 * me + 1, :], ["yjf"], ["r3"])
-                bulk_send(3)
-
-        def side5():
-            tt(al, PB[4][:, 0:S], T.nc[:], A.is_ge, ["p4", "nc"], [ak])
-            mm(PB[5][:, 0:S], IB, T.szb[:], True, False, ["shw", "szb"], "p5")
-            mm(PB[5][:, 0:S], T.i1k[:], al, False, False, ["i1k", ak], "p5")
-
-        side = {0: side0, 3: side1, 4: side2, 5: side4, 7: side3, 9: side5}
+            mms([(PB[3][:, 0:S], IB, T.ref[:], True, False, ["shw", "ref"], S), (PB[3][:, 0:S], T.i448[:], T.sl[:], False, True, ["i448", "sl"], S)], "p3")
+            lin(T.yrf[:], PB[3][:, 0:S], 1.0, col(17), ["p3", "pf17"], ["yrf"])
+            lin(T.yjf[:], jv, 1.0, col(18), [jk, "pf18"], ["yjf"])
+            dma("Y", "ds3", T.s3[:, 0:112, :], T.yrf[:], ["yrf"], ["s3"])
+            dma("Y", "ds3", T.s3[:, 112:119, :], T.yjf[0:128:16, :], ["yjf"], ["s3"])
+            dma("Y", "ds3", T.r3[me, 0:112, :], T.yrf[mine, :], ["yrf"], ["r3"])
+            dma("Y", "ds3", T.r3[me, 112:119, :], T.yjf[16 * me:16 * me + 1, :], ["yjf"], ["r3"])
+            bulk_send(3)
         for k in range(16):
-            act(T.gg[:, S * k:S * k + S], T.tab[:, 0:9 * S].indirect(T.lt[:, 28 * k:28 * k + 28]), F.Abs, TAB + ["lt", "bk"], ["gg%d" % k], bias=T.bk[:, k:k + 1])
-            if k == 0 and t > 1:
-                side0()
-            tt(T.ind[:, S * k:S * k + S], T.gg[:, S * k:S * k + S], PB[1][:, 0:S], A.is_gt, ["gg%d" % k, "p1"], ["ind%d" % k])
-            mm(PB[2][:, 0:S], T.uw[:, 15 - k:143 - k], T.ind[:, S * k:S * k + S], k == 0, k == 15, ["uw", "ind%d" % k], "p2")
-            if k == 0 and t > 1:
-                o = S * ((t - 1) % 2)
-                mm(PB[2][:, 0:S], T.i32[:], T.far[:, o:o + S], False, False, ["i32", "far%d" % ((t - 1) % 2)], "p2")
-            if k in side and not (k == 0 and t > 1):
-                side[k]()
+            c = slice(S * k, S * k + S)
+            aim = T.tab[:, 0:9 * S].indirect(T.lt[:, 28 * k:28 * k + 28])
+            if k < NA:
+                tt(T.ind[:, c], aim, T.gg[:, c], A.is_lt, TAB + ["lt%d" % k, "gg%d" % k], ["ind%d" % k], per=GAT)
+            else:
+                act(T.gg[:, c], aim, F.Abs, TAB + ["lt%d" % k, "bk"], ["gg%d" % k], per=GAT, bias=T.bk[:, k:k + 1])
+                tt(T.ind[:, c], T.gg[:, c], PB[1][:, 0:S], A.is_gt, ["gg%d" % k, "p1"], ["ind%d" % k])
+            count(T.uw[:, 15 - k:143 - k], T.ind[:, c], ["uw", "ind%d" % k])
+        far = T.far[:, o:o + S]
+        ts(far, PB[2][:, 0:S], col(14), 0.0, A.max, A.not_equal, ["p2", "pf14"], ["far%d" % (t % 2)])
+        mms([(PB[5][:, 0:S], T.b20[:], far, False, True, ["b20", "far%d" % (t % 2)], S)], "p5")
+        act(T.ln[:, 8:8 + S], PB[5][:, 0:S], F.Relu, ["p5"], ["ln", "tot%d" % t], S + 170, accum_out=T.tot[:, t:t + 1])
 
     for t in range(RO):
-        gap(t)
-        main(t + 1)
+        table(t)
+        test(t + 1)
+        if t + 1 < RO:
+            sums_send(t + 1, T.mw, "mw")
 
-    lengths(RO)
-    sums_send(RO, T.mf, "mf")
+    o = 64 * RO
+    dma("Y", "ds4", T.s4[:], T.far[:, 0:S], ["far0"], ["s4"])
+    dma("Y", "ds4", T.r4[me], T.far[mine, 0:S], ["far0"], ["r4"])
+    calls = []
+    for j in range(4):
+        c, out = slice(Q4 * j, Q4 * j + Q4), PB[1][0:Q4, 8 * j:8 * j + 8]
+        calls += [(out, T.jv[:, c], T.d64[:], True, False, ["jv0", "d64"], 8), (out, T.ncb[:, c], T.d65[:], False, False, ["ncb", "d65"], 8),
+                  (out, T.far[:, c], T.d20[:], False, True, ["far0", "d20"], 8)]
+    mms(calls, "p1")
+    for j in range(4):
+        ts(T.xs[0:Q4, o + j:o + 64:8], PB[1][0:Q4, 8 * j:8 * j + 8], 0.0, None, A.max, None, ["p1", "xz"], ["xc%d" % j], 16)
+    act(T.xs[:, o + 4:o + 64:8], T.ones[:, 0:8], F.Identity, ["ones", "xz", "tot%d" % RO], ["xc4"], 16, scale=T.tot[:, RO:RO + 1])
+    XC = keys("xc", 0, 5)
+    small_send(RO, XC)
     bulk_send(4)
+    cp(T.xr[:, o + 8 * me:o + 8 * me + 8], T.xs[:, o + 56:o + 64], XC, ["xo4"], 16)
     dma("Y", "do3", T.jrow[0:8, :], T.r3[:, 112:119, :], ["r3"], ["jrow"])
-    dma("Y", "do4", T.faro[:], T.r4[:], ["r4"], ["faro"])
-    dma("S", "dy", T.yr[:], T.r3[:, 0:112, :], ["r3"], ["yr"])
-    dma("S", "dy", T.yj[:], T.r3[:, 112:119, :], ["r3"], ["yj"])
-    ts(T.yjf[0:8, :], T.jrow[0:8, :], float(-S * me), None, A.add, None, ["jrow"], ["yjf"])
-    tt(T.al8[0:8, :], T.yjf[0:8, :], T.ion[0:8, :], A.is_equal, ["yjf", "ion"], ["al8"])
-    mm(PB[6][:, 0:S], IB, T.szob[:], True, False, ["shw", "szob"], "p6")
-    mm(PB[6][:, 0:S], T.rep[0:8, :], T.al8[0:8, :], False, False, ["rep", "al8"], "p6")
-    for q in order[::-1]:
-        src, o, k = (T.xs, 64 * RO + 8 * order.index(me), "xs") if q == me else (T.xr, 64 * RO + 8 * q, "xr")
-        mm(PB[7][:, 0:1], T.em[:], src[:, o:o + 1], q == me, False, ["em", k + str(RO)], "p7")
-        mm(PB[7][:, 0:1], T.ez[:, 112 - 16 * q:240 - 16 * q], src[:, o + 1:o + 2], False, q == order[0], ["ez", "ez0", k + str(RO)], "p7")
-    cp(T.yaf[:, 0:1], PB[7][:, 0:1], ["p7"], ["yaf0"])
-    mm(PB[6][:, 0:S], T.b20[:], T.faro[:], False, True, ["b20", "faro"], "p6")
-    act(T.ln[:], PB[6][:, 0:S], F.Relu, ["p6"], ["ln"], bias=-1024.0)
+    dma("Y", "dy", T.yr[:], T.r3[:, 0:112, :], ["r3"], ["yr"])
+    dma("Y", "dy", T.yj[:], T.r3[:, 112:119, :], ["r3"], ["yj"])
+    ts(PB[3][0:8, 0:S], T.jrow[0:8, :], float(-S * me), None, A.add, None, ["jrow"], ["p3"])
+    tt(T.al8[0:8, :], PB[3][0:8, 0:S], T.ion[0:8, :], A.is_equal, ["p3", "ion"], ["al8"])
+    mms([(PB[6][:, 0:S], IB, T.szob[:], True, False, ["shw", "szob"], S), (PB[6][:, 0:S], T.rep[0:8, :], T.al8[0:8, :], False, True, ["rep", "al8"], S)], "p6")
+    act(T.szal[:], PB[6][:, 0:S], F.Relu, ["p6"], ["szal"], bias=-1024.0)
+    mms([(PB[4][:, 0:S], IB, T.szal[:], True, False, ["shw", "szal"], S)], "p4")
+    XR = ["xr4", "xo4"]
+    mms([(PB[7][:, 0:8], T.ema[:], T.xr[:, o + 4:o + 64:8], True, True, ["ema"] + XR, 256),
+         (PB[7][:, 8:16], T.emb[:], T.xr[:, o + 4:o + 64:8], True, True, ["emb"] + XR, 256)], "p7")
+    for h in range(2):
+        lin(T.xe[:, 256 * h:256 * h + 256], T.xr[:, o:o + 64].indirect(T.xl[:, 16 * h:16 * h + 16]), 1.0, 0.0, XR + ["xl"], ["xe%d" % h], 256, GAT, "SV"[h])
+    tt(T.t16[:], PB[7][:, 0:16], T.mk[:], A.mult, ["p7", "mk", "mk0"], ["t16"], 16)
+    op("V", lambda: V.tensor_reduce(T.yaf[:, 0:1], T.t16[:], AX.X, A.add), ["t16"], ["yaf0"], 16)
+    mms([(PB[4][:, Q4 * j:Q4 * j + Q4], T.xe[0:Q4, 128 * j:128 * j + 128], T.shw[0:Q4, 128:128 + Q4], False, j == 3, ["shw", "xe%d" % (j // 2)], Q4) for j in range(4)], "p4")
+    op("V", lambda: V.tensor_tensor_scan(T.yaf[:, 1:S], T.ones[:, 0:S - 1], PB[4][:, 0:S - 1], T.yaf[:, 0:1], A.mult, A.add), ["ones", "p4", "yaf0"], ["yaf"])
+    dma("Y", "dz", T.ya[:], T.yaf[:], ["yaf", "yaf0"], ["ya"])
     dma("G", "dg", T.yf[:], T.r4[:], ["r4"], ["yf"])
-    op("V", lambda: V.tensor_tensor_scan(T.yaf[:, 1:S], T.ones[:, 0:S - 1], T.ln[:, 0:S - 1], T.yaf[:, 0:1], A.mult, A.add), ["ones", "ln", "yaf0"], ["yaf"])
-    dma("Y", "dy", T.ya[:], T.yaf[:], ["yaf", "yaf0"], ["ya"])
+    issue()
     for s in cnt:
         need("G", (s, None))

from concourse.bass import DstId, RemoteDMATransfer
from concourse.mybir import AluOpType as A, ActivationFunctionType as F, AxisListType as AX

N, S, RO = 8, 448, 4
W = N * S
CEN = 131072.0
K = 8781824.0
CPOS = 0.5 * K + CEN
CNEG = 1.5 * K + 1 + CEN
MID = 13800000.0
BIG = 33554432.0
MAG = 192.0
C0 = S * MAG - W - 224
NA = 3
Q4 = S // 4
PARTS = [(0, 3), (3, 10), (10, 16)]
PARTS0 = [(0, 5), (5, 10), (10, 16)]
BB = 6
CY, GAT = 0.00083, 1.56
XL, PASSES = 5.0, 6

SB = lambda n, d="float32": ("sbuf", [128, n], d)
H = "bfloat16"
SCRATCH = {
    "s0": ("dram", [N, 128, 8], "int32"), "r0": ("dram", [N, 128, 8], "int32"),
    "s1": ("dram", [N, 128, 56], H), "r1": ("dram", [N, 128, 56], H),
    "s5": ("dram", [N, 128, 112], H), "r5": ("dram", [N, 128, 112], H),
    "s2": ("dram", [N, 128, 112], H), "r2": ("dram", [N, 128, 112], H),
    "s3": ("dram", [N, 128, 64], "float32"), "r3": ("dram", [N, 128, 64], "float32"),
    "s4": ("dram", [N, 128, 56], H), "r4": ("dram", [N, 128, 56], H),
    "xs": SB(5 * 64), "xr": SB(5 * 64),
    "pi": SB(8, "int32"), "pf": SB(24), "ion": SB(S), "nc": SB(S), "ncb": SB(S, H), "tb": SB(S, H), "thr": SB(S), "ones": SB(S),
    "onesb": SB(S, H), "kv": SB(128, H), "cm": SB(128), "cdv": SB(128), "rv": SB(64), "gv": SB(64),
    "mw": SB(64), "mo": SB(64), "t64": SB(64), "u64": SB(64),
    "shw": SB(256, H), "ip": SB(128, H), "im": SB(128, H), "i16": SB(128, H), "i32": SB(128, H), "iw": SB(128, H),
    "nf": SB(128, H), "i448": SB(128, H), "na": SB(128, H), "nb": SB(128, H), "nd": SB(128, H), "ne": SB(128, H),
    "idf": SB(128), "ww": SB(144, H), "w1": SB(144, H), "uw": SB(144, H), "nlc": SB(28 * NA + 16, H),
    "b20": SB(128, H), "b512": SB(128, H), "em": SB(128), "ema": SB(128), "emb": SB(128), "rep": SB(128, H),
    "ct": SB(8), "sg": SB(16), "cv": SB(16), "t16": SB(16), "u16": SB(16), "mk": SB(16), "rot": SB(2, "uint16"),
    "d20": SB(8, H), "d64": SB(8, H), "d65": SB(8, H), "xf": SB(32), "xl": SB(32, "uint16"),
    "szo": SB(S, "int32"), "rfo": SB(S, "int32"), "szob": SB(S, H), "to": SB(S), "m2": SB(2 * S, H), "jrow": SB(S),
    "al8": SB(S, H), "szal": SB(S, H), "xe": SB(512, H), "yaf": SB(S),
    "cdo": SB(28, "int32"), "cdm": SB(28, "uint16"), "m5": SB(2 * S, H), "m6": SB(2 * S, H), "nth": SB(S, H), "cbo": SB(S, H), "sm": SB(S, H),
    "cdi": SB(28, "int32"), "rci": SB(16, "int32"), "szb": SB(S + 16, H),
    "cdl": SB(28, "uint16"), "bk": SB(16), "cb": SB(S, H), "lt": SB(S, "uint16"), "ol": SB(28 * NA + 16, "uint16"),
    "ln": SB(S + 8), "tot": SB(8), "hi": SB(S, H), "lw": SB(S, H), "g1": SB(16 * S, H),
    "tab": SB(9 * S), "jt": SB(9 * S, H), "gr": SB(16 * S, H), "gg": SB(16 * S), "ind": SB(16 * S, H),
    "bs": SB(8), "ro": SB(16), "c1": SB(16), "cs": SB(16), "ta": SB(S, H), "tc": SB(S),
    "ref": SB(S, H), "sl": SB(S, H), "neg": SB(S, H), "mis": SB(S, H),
    "jv": SB(2 * S, H), "far": SB(2 * S, H), "yrf": SB(S), "yjf": SB(S),
}
for _b in range(8):
    SCRATCH["p%d" % _b] = ("psum", [128, 512], "float32")
SEMAPHORES = (["cV", "cS", "cP", "cG", "out", "dg"] + ["m%d" % i for i in range(6)] + ["xr%d" % t for t in range(5)]
              + ["dsz", "drf", "dcd", "ds0", "dr0", "ds5", "dw5", "ds1", "dw1", "dw1b", "ds2", "dw2", "dw2b", "dj0", "dj1", "dj2",
                 "dn0", "dn1", "dn2", "ds3", "do3", "dy", "dz", "ds4"])


def plan(T, topo, r):
    me = T.cores[r]
    others = [d for d in range(N) if d != r]
    direct = [d for d in others if topo.may_write(me, T.cores[d])]
    away = [d for d in others if d not in direct]
    able = [c for c in topo.cores_of(me) if c != me and all(topo.may_write(c, T.cores[d]) for d in away)]
    bulk = {d: able[i % len(able)] for i, d in enumerate(away)}
    per = N // len(able)
    small = [(c, (away + direct)[i * per:(i + 1) * per]) for i, c in enumerate(able)]
    return direct, away, bulk, small


def bits(engs):
    m = 0
    for e in engs:
        m |= 1 << e
    return m


def share(engs, parts):
    n = 1
    while 2 * n * parts <= len(engs):
        n *= 2
    return [engs[i * n:(i + 1) * n] for i in range(parts)]


def xfer(topo, src, dst, a, b, engs, sem):
    rid, pid = topo.addr(dst, src)
    return RemoteDMATransfer(dst_ids=[DstId(rid=rid, pnc=pid)], dma_engine_mask=bits(engs), remote_sem=sem, src=a, dst=b)


def split(T, topo, r):
    me = T.cores[r]
    direct, away, bulk, small = plan(T, topo, r)
    off = topo.engines(me, T.cores[direct[0]])
    on = [e for e in topo.engines(me, small[0][0]) if e not in off]
    return off, on


ORDER = ["m0", "m1", "m2", "x0", "m5", "x1", "x2", "x3", "m3", "x4", "m4"]


def helper(g, core, T, topo):
    rs = [r for r in range(N) if core in topo.cores_of(T.cores[r])]
    if not rs:
        return
    r = rs[0]
    direct, away, bulk, small = plan(T, topo, r)
    off, on = split(T, topo, r)
    mine = [d for d in away if bulk[d] == core]
    few = [ds for c, ds in small if c == core]
    sent = 0
    for m in ORDER:
        if m[0] == "m" and mine:
            buf = T["r" + m[1]]
            g.wait_ge(T.sem[m], len(share(on, len(away))[0]) * len(mine))
            es = share(topo.engines(core, T.cores[mine[0]]), len(mine))
            g.remote_dma_fused([xfer(topo, core, T.cores[d], buf[d], buf[r], e, T.sem[m]) for d, e in zip(mine, es)], local_sem=T.sem.out)
            sent += sum(len(e) for e in es)
        if m[0] == "x" and few:
            t = int(m[1]); ds = few[0]
            g.wait_ge(T.sem["xr%d" % t], len(share(on + off, len(small))[0]))
            es = share(topo.engines(core, T.cores[ds[0]]), len(ds))
            g.remote_dma_fused([xfer(topo, core, T.cores[d], T.xs[:, 64 * t + 8 * i:64 * t + 8 * i + 8],
                                     T.xr[:, 64 * t + 8 * r:64 * t + 8 * r + 8], e, T.sem["xr%d" % t])
                                for i, (d, e) in enumerate(zip(ds, es))], local_sem=T.sem.out)
            sent += sum(len(e) for e in es)
    if sent:
        g.wait_ge(T.sem.out, sent)


def rank_program(g, core, T, topo):
    me = T.rank_of(core)
    if me is None:
        return helper(g, core, T, topo)
    direct, away, bulk, small = plan(T, topo, me)
    off, on = split(T, topo, me)
    order = away + direct + [me]
    Q = {"V": g.vector, "S": g.scalar, "P": g.tensor, "G": g, "Y": g.sync}
    V, Sc, P = g.vector, g.scalar, g.tensor

    cnt, seen, wr, rd = {}, {}, {}, {}

    def need(e, tok):
        s, v = tok
        if v is None:
            v = cnt[s]
        assert v <= cnt[s], (e, tok)
        if seen.get((e, s), 0) < v:
            Q[e].wait_ge(T.sem[s], v)
            seen[(e, s)] = v

    def deps(e, reads, writes):
        for k in reads:
            for t in wr.get(k, []):
                need(e, t)
            if k[0] == "p" and k[1:].isdigit():
                for o, t in rd.get(k, {}).items():
                    if o != e:
                        need(e, t)
        for k in writes:
            for t in wr.get(k, []):
                if not (e == "P" and t[0] == "cP"):
                    need(e, t)
            for o, t in rd.get(k, {}).items():
                need(e, t)

    def note(e, tok, reads, writes, add=False):
        for k in reads:
            rd.setdefault(k, {})[e if tok[0][0] == "c" else tok[0]] = tok
        for k in writes:
            wr[k] = (wr.get(k, []) if add else []) + [tok]
            if not add:
                rd[k] = {}

    def op_now(e, fn, reads, writes, inc=True):
        deps(e, reads, writes)
        ins = fn()
        s = "c" + e
        if inc:
            cnt[s] = cnt.get(s, 0) + 1
            ins.then_inc(T.sem[s], 1)
            note(e, (s, cnt[s]), reads, writes)
        else:
            note(e, (s, cnt.get(s, 0) + 1), reads, writes)

    def dma_now(e, sem, out, in_, reads, writes):
        fresh = [k for k in writes if (sem, None) not in wr.get(k, [])]
        deps(e, reads, fresh)
        Q[e].dma_start(out, in_).then_inc(T.sem[sem], 16)
        cnt[sem] = cnt.get(sem, 0) + 16
        note(e, (sem, None), reads, fresh)

    def arrive(sem, n, key, add=False):
        cnt[sem] = n
        note("G", (sem, n), [], [key], add)

    def fused(xs, reads, n):
        deps("G", reads, [])
        g.remote_dma_fused(xs, local_sem=T.sem.out)
        cnt["out"] = cnt.get("out", 0) + n

    def bulk_now(i):
        s, r, sem = T["s%d" % i], T["r%d" % i], "m%d" % i
        ea, eb = share(off, len(direct)), share(on, len(away))
        xs = [xfer(topo, core, bulk[d], s[d], r[d], e, T.sem[sem]) for d, e in zip(away, eb)]
        xs += [xfer(topo, core, T.cores[d], s[d], r[me], e, T.sem[sem]) for d, e in zip(direct, ea)]
        fused(xs, ["s%d" % i], sum(len(e) for e in ea + eb))
        n = 0
        for q in range(N):
            if q != me:
                dq, aq, bq, sq = plan(T, topo, q)
                if me in dq:
                    n += len(share(split(T, topo, q)[0], len(dq))[0])
                else:
                    n += len(share(topo.engines(bq[me], core), sum(1 for d in aq if bq[d] == bq[me]))[0])
        arrive(sem, n, "r%d" % i, True)

    def small_now(t, reads):
        eb = share(on + off, len(small))
        cols = 64 // len(small)
        xs = []
        for (c, ds), e in zip(small, eb):
            o = 64 * t + 8 * order.index(ds[0])
            xs.append(xfer(topo, core, c, T.xs[:, o:o + cols], T.xs[:, 64 * t:64 * t + cols], e, T.sem["xr%d" % t]))
        fused(xs, reads, sum(len(e) for e in eb))
        nr = 0
        for q in range(N):
            if q != me:
                c, ds = [x for x in plan(T, topo, q)[3] if me in x[1]][0]
                nr += len(share(topo.engines(c, core), len(ds))[0])
        arrive("xr%d" % t, nr, "xr%d" % t)

    nodes, lastw, readers, held, batch, mates = [], {}, {}, {}, {}, {}
    wide = [S]

    def node(engs, fn, reads, writes, dur, lat=0.0, adds=()):
        i = len(nodes)
        pre = set()
        for k in reads:
            pre.update(lastw.get(k, []))
            if k[0] == "p" and k[1:].isdigit():
                pre.update(j for j in readers.get(k, []) if nodes[j][0] != engs or len(engs) > 1)
        for k in list(writes) + list(adds):
            pre.update(readers.get(k, []))
            pre.update(j for j in lastw.get(k, []) if k in writes or k not in nodes[j][5])
        for k in reads:
            readers.setdefault(k, []).append(i)
        for k in writes:
            lastw[k], readers[k] = [i], []
        for k in adds:
            if readers.get(k) or not all(k in nodes[j][5] for j in lastw.get(k, [])):
                held[k] = set(readers.get(k, [])) | set(lastw.get(k, []))
                lastw[k], readers[k] = [], []
            pre.update(held.get(k, ()))
            lastw.setdefault(k, []).append(i)
        for j in list(pre):
            pre.update(mates.get(j, ()))
        pre.discard(i)
        nodes.append((engs, fn, pre, dur, lat, set(adds)))

    def op(e, fn, reads, writes, n=None, per=1.0):
        n = wide[0] if n is None else n
        fix = {"V": 0.05, "S": 0.065, "G": 0.13}
        node(e, lambda x: op_now(x, fn if len(e) == 1 else (lambda: fn(x)), reads, writes), reads, writes,
             {x: fix[x] + max(n * per, 16) * CY for x in e}, 0.06)

    def dma(e, sem, out, in_, reads, writes, lat=1.9, now=False):
        if now:
            dma_now(e, sem, out, in_, reads, writes)
            node("", None, reads, [], {}, lat, adds=list(writes))
        else:
            node(e, lambda x: dma_now(e, sem, out, in_, reads, writes), reads, [], {e: 0.06 if e != "G" else 1.5}, lat, adds=list(writes))
        batch.setdefault(sem, []).append(len(nodes) - 1)
        mates[len(nodes) - 1] = batch[sem]

    def remote(fn, reads, key, lat):
        first = "gq" not in lastw
        node("G", lambda x: fn(), reads, ["gq", "sent" + key], {"G": 2.8 if first else 0.6}, 0.0)
        node("", None, ["sent" + key], [], {}, lat + (2.4 if first else 0), adds=[key])

    def mms(calls, bank, adds=False):
        reads = sorted({k for c in calls for k in c[5]})

        def now(x):
            for j, (out, l, r, st, sp, ks, n) in enumerate(calls):
                if adds:
                    st, sp = adds()
                op_now("P", lambda: P.matmul(out, l, r, st, sp), ks, [bank], j == len(calls) - 1)
        node("P", now, reads, [] if adds else [bank], {"P": sum(max(64, c[6]) for c in calls) * CY / 2}, 0.12, adds=[bank] if adds else [])

    def issue():
        n = len(nodes)
        pre = [nd[2] for nd in nodes]
        post = [[] for _ in range(n)]
        for i in range(n):
            for j in pre[i]:
                post[j].append(i)

        def lay(seq, before, back):
            busy = {x: [] for x in "VSPGY"}
            fin, start, eng = [0.0] * n, [0.0] * n, [""] * n
            for i in seq:
                engs, fn, _, dur, lat, _ = nodes[i]
                r = max((fin[j] for j in before[i]), default=0.0) + (lat if back else 0.0)
                best = (r, r, "", 0)
                for x in engs:
                    t, at = r, len(busy[x])
                    while at and busy[x][at - 1][1] > t:
                        at -= 1
                    while at < len(busy[x]) and busy[x][at][0] < t + dur[x]:
                        t = max(t, busy[x][at][1])
                        at += 1
                    if not best[2] or t + dur[x] < best[1]:
                        best = (t, t + dur[x], x, at)
                start[i], end, eng[i], at = best
                if eng[i]:
                    busy[eng[i]].insert(at, (start[i], end))
                fin[i] = end + (0.0 if back else lat)
            return fin, start, eng

        seq, kept = list(range(n)), None
        for _ in range(PASSES):
            fin, start, eng = lay(seq, pre, False)
            if kept is None or max(fin) < kept[0]:
                kept = (max(fin), start, eng)
            fin = lay(sorted(range(n), key=lambda i: (-fin[i], -i)), post, True)[0]
            seq = sorted(range(n), key=lambda i: (-fin[i], i))
        for i in sorted(range(n), key=lambda i: (kept[1][i], i)):
            if kept[2][i]:
                nodes[i][1](kept[2][i])

    def bulk_send(i):
        remote(lambda: bulk_now(i), ["s%d" % i], "r%d" % i, XL + 0.5)

    def small_send(t, reads):
        remote(lambda: small_now(t, reads), reads, "xr%d" % t, XL + (1.0 if t == 0 else 0.0))

    def sums_send(t, mask, mk):
        act(T.xs[:, 64 * t:64 * t + 64], mask[:], F.Identity, [mk, "tot%d" % t], ["xs%d" % t], 64, scale=T.tot[:, t:t + 1])
        small_send(t, ["xs%d" % t])
        lin(T.xr[:, 64 * t + 8 * me:64 * t + 8 * me + 8], mask[:, 56:64], T.tot[:, t:t + 1], 0.0, [mk, "tot%d" % t], ["xo%d" % t], 16)

    def ts(out, in0, s1, s2, o0, o1, reads, writes, n=None, per=1.0):
        if o1 is None:
            op("V", lambda: V.tensor_scalar(out, in0, s1, None, o0), reads, writes, n, per)
        else:
            op("V", lambda: V.tensor_scalar(out, in0, s1, s2, o0, o1), reads, writes, n, per)

    def tt(out, a, b, o, reads, writes, n=None, per=1.0):
        op("V", lambda: V.tensor_tensor(out, a, b, o), reads, writes, n, per)

    def cp(out, a, reads, writes, n=None, per=1.0):
        op("V", lambda: V.tensor_copy(out, a), reads, writes, n, per)

    def ms(out, v, writes, n=None):
        op("V", lambda: V.memset(out, v), [], writes, n)

    def act(out, a, f, reads, writes, n=None, per=1.0, **kw):
        op("S", lambda: Sc.activation(out, a, f, **kw), reads, writes, n, per)

    def lin(out, a, scale, bias, reads, writes, n=None, per=1.0, e="VS"):
        def fn(x=e):
            if x == "S":
                return Sc.activation(out, a, F.Identity, scale=scale, bias=bias)
            return V.tensor_scalar(out, a, scale, bias, A.mult, A.add)
        op(e, fn, reads, writes, n, per)

    def iota(out, pat, base, chm, key, n, flt=True):
        if flt:
            op("G", lambda: g.iota(out, pat, base, chm, allow_small_or_imprecise_dtypes=True), [], [key], n, 2)
        else:
            op("G", lambda: g.iota(out, pat, base, chm), [], [key], n, 2)

    PB = [T["p%d" % b] for b in range(8)]
    mine = slice(16 * me, 16 * me + 16)
    col = lambda j: T.pf[:, j:j + 1]
    pp, pm, pd = col(0), col(1), col(2)
    IB = T.shw[:, 128:256]
    SZ = T.szb[:, 16:16 + S]
    JT = ["jt%d" % j for j in range(9)]
    TAB = ["tab%d" % j for j in range(9)]
    GV = ["gv%d" % i for i in range(N)]

    dma("Y", "ds0", T.s0[:, 0:56, :], T.cd[:], [], ["s0"], 1.3, True)
    dma("S", "ds0", T.s0[:, 56:88, :], T.rch[:], [], ["s0"], 1.3, True)
    dma("S", "ds0", T.s0[:, 88:128, :], T.sz[0:8, 0:320], [], ["s0"], 1.3, True)
    dma("Y", "dsz", T.szo[:], T.sz[:], [], ["szo"], 2.2, True)
    dma("S", "drf", T.rfo[:], T.rf[:], [], ["rfo"], 3.0, True)
    dma("Y", "dr0", T.r0[me, 0:56, :], T.cd[mine, :], [], ["r0"], 3.2, True)
    dma("Y", "dr0", T.r0[me, 56:88, :], T.rch[mine, :], [], ["r0"], 3.2, True)
    dma("Y", "dcd", T.cdo[:], T.cd[:], [], ["cdo"], 3.3, True)
    iota(T.pi[:, 0:1], [[0, 1]], 0, 1, "pi", 1, False)
    iota(T.ion[:], [[1, S]], 0, 0, "ion", S)
    iota(T.rv[:], [[0, 8], [1, 8]], 0, 0, "rv", 64)
    iota(T.cdv[:], [[1, 8], [0, 16]], 0, 0, "cdv", 128)
    iota(T.cm[:], [[0, 8], [1, 16]], 0, 0, "cm", 128)
    iota(T.xf[:], [[1, 4], [8, 8]], 0, 0, "xf", 32)
    iota(T.thr[:], [[0, 16], [16, 28]], int(W + C0), 0, "thr", S)
    wide[0] = 16
    for i, d in enumerate(order):
        ms(T.gv[:, 8 * i:8 * i + 8], float(d), ["gv%d" % i])
    ts(T.pi[:, 1:2], T.pi[:, 0:1], 15, None, A.bitwise_and, None, ["pi"], ["pi1"])
    ts(T.pi[:, 2:3], T.pi[:, 0:1], 4, None, A.arith_shift_right, None, ["pi"], ["pi2"])
    ts(T.pi[:, 3:4], T.pi[:, 0:1], 1, None, A.arith_shift_right, None, ["pi"], ["pi3"])
    ts(T.pi[:, 6:7], T.pi[:, 0:1], 1, None, A.bitwise_and, None, ["pi"], ["pi6"])
    cp(T.pf[:, 0:4], T.pi[:, 0:4], ["pi", "pi1", "pi2", "pi3"], ["pf"])
    cp(col(4), T.pi[:, 6:7], ["pi6"], ["pf4"])
    tt(T.pi[:, 4:5], T.pi[:, 1:2], T.pi[:, 2:3], A.add, ["pi1", "pi2"], ["pi4"])
    ts(T.pi[:, 5:6], T.pi[:, 4:5], 7, None, A.bitwise_and, None, ["pi4"], ["pi5"])
    cp(T.rot[:, 0:1], T.pi[:, 5:6], ["pi5"], ["rot"])
    cp(T.xl[:], T.xf[:], ["xf"], ["xl"])
    ms(T.szb[:, 0:16], 0.0, ["sz0"])
    ms(T.ln[:, 0:8], 0.0, ["ln0"])
    ts(col(5), pm, 1.0, None, A.is_equal, None, ["pf"], ["pf5"])
    ts(col(7), pm, 0.0, None, A.is_equal, None, ["pf"], ["pf7"])
    ts(col(11), pm, float(NA), None, A.is_ge, None, ["pf"], ["pf11"])
    ts(col(19), pd, float(me), None, A.is_lt, None, ["pf"], ["pf19"])
    ts(col(20), pd, float(me), None, A.is_equal, None, ["pf"], ["pf20"])
    for j, src, sk, a, b in ((6, pd, "pf", 16.0, 15.0), (8, col(5), "pf5", float(S), col(7)), (9, col(3), "pf", 16.0, 15.0),
                             (10, col(4), "pf4", S - 1.0, 1.0), (12, col(11), "pf11", 2 * BIG, -BIG), (21, col(11), "pf11", -2 * BIG, BIG),
                             (13, col(11), "pf11", -S * MAG - 0.5, 0.5), (14, col(11), "pf11", -1000.0, 0.0), (15, col(11), "pf11", float(-S), 0.0),
                             (16, col(11), "pf11", -1.0, 0.0), (17, pd, "pf", float(S), -C0 - W), (18, pd, "pf", float(S), 224.0)):
        lin(col(j), src, a, b, [sk, "pf7"], ["pf%d" % j])
    ts(T.u16[:], T.ion[:, 0:16], pd, 8.0, A.add, A.is_ge, ["ion", "pf"], ["u16"])
    lin(T.cv[:], T.u16[:], -8.0, MAG, ["u16"], ["cv"])
    tt(T.cv[:], T.cv[:], T.ion[:, 0:16], A.add, ["cv", "ion"], ["cv"])
    lin(T.cv[:], T.cv[:], col(5), 0.0, ["cv", "pf5"], ["cv"])
    lin(T.sg[:], T.u16[:], 2.0, -1.0, ["u16"], ["sg"])
    ts(T.ct[:], T.ion[:, 0:8], pd, CNEG, A.is_lt, A.mult, ["ion", "pf"], ["ct"])
    ts(T.t16[:, 0:8], T.ion[:, 0:8], pd, CPOS, A.is_gt, A.mult, ["ion", "pf"], ["t16"])
    lin(T.ct[:], T.ct[:], 1.0, -MID, ["ct"], ["ct"])
    tt(T.ct[:], T.ct[:], T.t16[:, 0:8], A.add, ["ct", "t16"], ["ct"])
    ts(T.d20[:], T.gv[:, 0:64:8], pd, 20.0, A.is_equal, A.mult, GV + ["pf"], ["d20"])
    lin(T.d64[:], T.d20[:], 3.2, 0.0, ["d20"], ["d64"])
    lin(T.d65[:], T.d20[:], -3.2, 0.0, ["d20"], ["d65"])
    lin(T.mk[:, 0:8], T.ion[:, 0:8], 0.0, 1.0, ["ion"], ["mk0"])
    ts(T.mk[:, 8:16], T.ion[:, 0:8], pd, None, A.is_lt, None, ["ion", "pf"], ["mk"])
    wide[0] = 64
    ms(T.xs[:, 64 * RO:64 * RO + 64], 0.0, ["xz"])
    for m, mk, a, b in ((T.mo, "mo", float(me), pd), (T.mw, "mw", pd, float(me))):
        ts(m[:], T.rv[:], a, None, A.is_gt, None, ["rv", "pf"], [mk])
        ts(T.t64[:], T.gv[:], b, None, A.is_gt, None, GV + ["pf"], ["t64"])
        ts(T.u64[:], T.rv[:], a, None, A.is_equal, None, ["rv", "pf"], ["u64"])
        tt(T.t64[:], T.t64[:], T.u64[:], A.mult, ["t64", "u64"], ["t64"], per=2)
        tt(m[:], m[:], T.t64[:], A.add, [mk, "t64"], [mk], per=2)
    wide[0] = 128
    ts(T.shw[:, 128:256], T.ion[:, 0:128], pp, None, A.is_equal, None, ["ion", "pf"], ["shw"])
    ts(T.em[:], T.cm[:], pm, None, A.is_equal, None, ["cm", "pf"], ["em"])
    ts(T.b512[:], T.cdv[:], pd, 512.0, A.is_equal, A.mult, ["cdv", "pf"], ["b512"])
    ts(T.rep[:], T.cdv[:], pp, 1024.0, A.is_equal, A.mult, ["cdv", "pf"], ["rep"])
    ts(T.uw[:], T.ion[:, 0:144], col(6), None, A.is_equal, None, ["ion", "pf6"], ["uw"])
    ts(T.w1[:], T.ion[:, 0:144], col(9), col(10), A.is_equal, A.mult, ["ion", "pf9", "pf10"], ["w1"])
    lin(T.ww[:], T.uw[:], col(8), 0.0, ["uw", "pf8"], ["ww"])
    lin(T.b20[:], T.b512[:], 20.0 / 512, 0.0, ["b512"], ["b20"])
    lin(T.kv[:], IB, 0.0, K + CEN, ["shw"], ["kv"])
    for out, key, sc, sk in ((T.shw[:, 0:128], "shw0", -1.0, "shw"), (T.idf[:], "idf", 1.0, "shw"), (T.iw[:], "iw", float(-W), "shw"), (T.ip[:], "ip", BIG, "shw"),
                             (T.im[:], "im", -BIG, "shw"), (T.i16[:], "i16", -16.0, "shw"), (T.i32[:], "i32", 32.0, "shw"), (T.i448[:], "i448", float(S), "shw"),
                             (T.na[:], "na", col(11), "pf11"), (T.nb[:], "nb", col(15), "pf15"), (T.nd[:], "nd", col(16), "pf16"),
                             (T.ne[:], "ne", col(12), "pf12"), (T.nf[:], "nf", col(21), "pf21")):
        lin(out, IB, sc, 0.0, ["shw", sk], [key])
    lin(T.ema[:], T.em[:], col(19), 0.0, ["em", "pf19"], ["ema"])
    lin(T.emb[:], T.em[:], col(20), 0.0, ["em", "pf20"], ["emb"])
    wide[0] = S
    lin(T.ones[:], T.ion[:], 0.0, 1.0, ["ion"], ["ones"])
    lin(T.onesb[:], T.ion[:], 0.0, 1.0, ["ion"], ["onesb"])
    lin(T.nc[:], T.ion[:], 1.0, -224.0, ["ion"], ["nc"])
    lin(T.ncb[:], T.ion[:], 1.0, -224.0, ["ion"], ["ncb"])
    lin(T.thr[:], T.thr[:], 1.0, pm, ["thr", "pf"], ["thr"])
    if NA:
        lin(T.nlc[:, 0:28 * NA], T.thr[:, 0:28 * NA], 1.0, -(W + C0 + 224.0), ["thr"], ["nlc"], 28 * NA)
    for j in range(9):
        lin(T.jt[:, S * j:S * j + S], T.ion[:], 0.0, T.cv[:, j:j + 1], ["ion", "cv"], ["jt%d" % j])
    bulk_send(0)
    cp(T.szob[:], T.szo[:], ["szo"], ["szob"])
    dma("Y", "ds1", T.s1[:], T.szob[:], ["szob"], ["s1"])
    dma("Y", "ds1", T.r1[me], T.szob[mine, :], ["szob"], ["r1"])
    bulk_send(1)
    ts(T.m2[:, S:2 * S], T.rfo[:], 1.0 / S, MAG - me - 223.5 / S, A.mult, A.add, ["rfo"], ["m2b"])
    ts(PB[2][:, 0:S], T.m2[:, S:2 * S], float(-S), S * (MAG - me) - 224.0, A.mult, A.add, ["m2b"], ["p2"])
    tt(T.m2[:, 0:S], T.rfo[:], PB[2][:, 0:S], A.add, ["rfo", "p2"], ["m2a"])
    dma("Y", "ds2", T.s2[:, 64:128, :], T.m2[:, S:2 * S], ["m2b"], ["s2"])
    dma("Y", "ds2", T.r2[me, 64:128, :], T.m2[mine, S:2 * S], ["m2b"], ["r2"])
    dma("Y", "ds2", T.s2[:, 0:64, :], T.m2[:, 0:S], ["m2a"], ["s2"])
    dma("Y", "ds2", T.r2[me, 0:64, :], T.m2[mine, 0:S], ["m2a"], ["r2"])
    bulk_send(2)
    act(T.to[:], T.szob[:], F.Identity, ["szob"], ["to", "tot0"], accum_out=T.tot[:, 0:1])
    sums_send(0, T.mo, "mo")
    cp(T.cdm[:], T.cdo[:], ["cdo"], ["cdm"], 28)
    lin(T.cbo[:], T.nc[:, 0:S].indirect(T.cdm[:, 0:28]), 1.0, 0.0, ["nc", "cdm"], ["cbo"], per=GAT)
    lin(T.m6[:, S:2 * S], T.m2[:, S:2 * S], 1.0, 0.0, ["m2b"], ["m6b"], e="S")
    lin(T.m6[:, 0:S], T.m2[:, 0:S], 1.0, 0.0, ["m2a"], ["m6a"], e="S")
    tt(T.sm[:], T.m2[:, S:2 * S].indirect(T.cdm[:, 0:28]), T.m6[:, S:2 * S], A.not_equal, ["m2b", "m6b", "cdm"], ["sm"], per=GAT)
    tt(T.mis[:], T.m2[:, 0:S].indirect(T.cdm[:, 0:28]), T.m6[:, 0:S], A.not_equal, ["m2a", "m6a", "cdm"], ["mis"], per=GAT)
    mms([(PB[3][:, 0:S], IB, T.cbo[:], True, False, ["shw", "cbo"], S), (PB[3][:, 0:S], T.b512[:], T.sm[:], False, True, ["b512", "sm"], S)], "p3")
    mms([(PB[4][:, 0:S], IB, T.cbo[:], True, False, ["shw", "cbo"], S), (PB[4][:, 0:S], T.b512[:], T.sm[:], False, False, ["b512", "sm"], S),
         (PB[4][:, 0:S], T.b512[:], T.mis[:], False, True, ["b512", "mis"], S)], "p4")
    ts(T.m5[:, S:2 * S], PB[3][:, 0:S], 224.0, None, A.min, None, ["p3"], ["m5b"])
    tt(T.m5[:, 0:S], PB[4][:, 0:S], T.nc[:], A.min, ["p4", "nc"], ["m5a"])
    dma("Y", "ds5", T.s5[:, 64:128, :], T.m5[:, S:2 * S], ["m5b"], ["s5"])
    dma("Y", "ds5", T.r5[me, 64:128, :], T.m5[mine, S:2 * S], ["m5b"], ["r5"])
    dma("Y", "ds5", T.s5[:, 0:64, :], T.m5[:, 0:S], ["m5a"], ["s5"])
    dma("Y", "ds5", T.r5[me, 0:64, :], T.m5[mine, 0:S], ["m5a"], ["r5"])
    bulk_send(5)
    dma("Y", "ds3", T.s3[:, 119:128, :], T.ion[0:72, 0:64], ["ion"], ["s3"])
    dma("Y", "dw1b", T.rci[:], T.r0[:, 56:88, :], ["r0"], ["rci"])
    dma("Y", "dw1b", T.cdi[:], T.r0[:, 0:56, :], ["r0"], ["cdi"])
    dma("Y", "dw1", SZ, T.r1[:], ["r1", "sz0"], ["szb"])
    dma("Y", "dw2", T.g1[0:16, :], T.r2[:], ["r2"], ["g1"])
    dma("Y", "dw2b", T.ref[:], T.r2[:, 0:64, :], ["r2"], ["ref"])
    dma("Y", "dw2b", T.sl[:], T.r2[:, 64:128, :], ["r2"], ["sl"])
    dma("Y", "dw5", T.jv[:, S:2 * S], T.r5[:, 0:64, :], ["r5"], ["jv1"])
    dma("Y", "dw5", T.cb[:], T.r5[:, 64:128, :], ["r5"], ["cb"])
    cp(T.cdl[:], T.cdi[:], ["cdi"], ["cdl"], 28)
    if NA:
        ts(T.bk[:, 0:NA], T.rci[:, 0:NA], -1.0, None, A.mult, None, ["rci"], ["bka"], 16)
    ts(T.bk[:, NA:16], T.rci[:, NA:16], -0.5 * K, None, A.add, None, ["rci", "bka"], ["bk"], 16)

    def JV(t):
        return T.jv[:, S * (t % 2):S * (t % 2) + S]

    def keys(name, a, b):
        return [name + str(k) for k in range(a, b)]

    def rename(k):
        lin(T.gr[:, S * k:S * k + S], T.jt[:, 0:9 * S].indirect(T.lt[:, 28 * k:28 * k + 28]), 1.0, 0.0, JT + ["lt%d" % k], ["gr%d" % k], per=GAT)

    def listed(t, a, b):
        c, n = slice(28 * a, 28 * b), 28 * (b - a)
        if t:
            mms([(PB[0][:, c], T.ww[:, 15 - q:143 - q], T.gr[:, S * a + q:S * b:16], q == 0, q == 15, ["ww"] + keys("gr", a, b), n) for q in range(16)], "p0")
        else:
            mms([(PB[0][:, c], T.w1[0:16, 15 - q:143 - q], T.g1[0:16, S * a + q:S * b:16], q == 0, q == 15,
                  ["w1", "g1"] + (["tab%d" % BB] if a else []), n) for q in range(16)], "p0")
        tt(T.ta[:, c], PB[0][:, c], T.thr[:, c], A.is_ge, ["p0", "thr"], keys("ta", a, b), n)
        ts(T.tb[:, c], T.ta[:, c], float(-W), None, A.mult, None, keys("ta", a, b), keys("tb", a, b), n, 0.5)
        tt(T.tc[:, c], PB[0][:, c], T.tb[:, c], A.add, ["p0"] + keys("tb", a, b), keys("tc", a, b), n)
        ts(T.lt[:, c], T.tc[:, c], -C0, None, A.add, None, keys("tc", a, b), keys("lt", a, b), n)

    def slot(j):
        l = T.shw[:, 16 * j:16 * j + 128]
        mms([(PB[j][:, 0:S], l, T.hi[:], True, False, ["shw", "shw0", "hi"], S)], "p%d" % j)
        mms([(PB[j][:, 0:S], l, T.lw[:], False, True, ["shw", "shw0", "lw"], S)], "p%d" % j)

    def limit(k):
        lin(T.gg[:, S * k:S * k + S], T.tab[:, 0:9 * S].indirect(T.ol[:, 28 * k:28 * k + 28]), 1.0, T.bk[:, k:k + 1], TAB + ["ol", "bk"], ["gg%d" % k], per=GAT)

    def table(t):
        src, sk = (T.ln[:, 7:7 + S], ["ln", "ln0"]) if t else (T.szb[:, 15:15 + S], ["szb", "sz0"])
        op("V", lambda: V.tensor_tensor_scan(PB[7][:, 0:S], T.ones[:], src, -CEN, A.mult, A.add), ["ones"] + sk, ["p7"])
        cp(T.hi[:], PB[7][:, 0:S], ["p7"], ["hi"])
        tt(T.lw[:], PB[7][:, 0:S], T.hi[:], A.subtract, ["p7", "hi"], ["lw"])
        lin(T.tab[:, 0:S], PB[7][:, 0:S], -1.0, -CPOS, ["p7"], ["tab0"])
        lin(T.tab[:, 8 * S:9 * S], PB[7][:, 0:S], 1.0, CNEG, ["p7"], ["tab8"])
        if t:
            for k in range(16):
                rename(k)
            dma("Y", "dn%d" % (t - 1), T.ref[:], T.gr[0:128:16, :], keys("gr", 0, 16), ["ref"])
            dma("Y", "dn%d" % (t - 1), T.nth[:], T.gr[0:128:16, :], keys("gr", 0, 16), ["nth"], 2.3)
        for a, b in (PARTS if t else PARTS0[:1]):
            listed(t, a, b)
        if NA:
            mms([(PB[7][:, 0:28 * NA], IB, T.nlc[:, 0:28 * NA], True, False, ["shw", "nlc"], 28 * NA),
                 (PB[7][:, 0:28 * NA], T.iw[:], T.ta[:, 0:28 * NA], False, True, ["iw"] + keys("ta", 0, NA), 28 * NA)], "p7")
            ts(T.ol[:, 0:28 * NA], PB[7][:, 0:28 * NA], W + 224.0, None, A.add, None, ["p7"], ["ol"], 28 * NA)
        for j in range(1, 8):
            if j != BB:
                slot(j)
        if t:
            for k in range(NA):
                limit(k)
        o, b = 64 * t, BB
        tt(T.t64[:, 0:32], T.xr[:, o:o + 32], T.xr[:, o + 32:o + 64], A.add, ["xr%d" % t, "xo%d" % t], ["t64"], 64)
        tt(T.u64[:, 0:16], T.t64[:, 0:16], T.t64[:, 16:32], A.add, ["t64"], ["u64"], 32)
        tt(T.t64[:, 0:8], T.u64[:, 0:8], T.u64[:, 8:16], A.add, ["u64"], ["t64"], 16)
        mms([(PB[b][:, S:S + 8], T.idf[:], T.ct[:], True, False, ["idf", "ct"], 256),
             (PB[b][:, S:S + 8], T.em[:], T.t64[:, 0:8], False, True, ["em", "t64"], 256)], "p%d" % b)
        cp(T.bs[:], PB[b][:, S:S + 8], ["p%d" % b], ["bs"], 16)
        slot(b)
        cp(T.ro[:], T.bs[:, 0:8].indirect(T.rot[:, 0:1]), ["bs", "rot"], ["ro"], 25)
        ts(T.c1[:], T.ro[:], T.ro[:, 0:1], CPOS, A.subtract, A.max, ["ro"], ["c1"], 16)
        tt(T.cs[:], T.c1[:], T.sg[:], A.mult, ["c1", "sg"], ["cs"], 32)
        for j in range(1, 8):
            lin(T.tab[:, S * j:S * j + S], PB[j][:, 0:S], 1.0, T.cs[:, j:j + 1], ["p%d" % j, "cs"], ["tab%d" % j])
        if not t:
            for k in range(NA):
                limit(k)
        dead = [(PB[1][:, 0:S], T.ip[:], T.ncb[:], True, False, ["ip", "ncb"], S), (PB[1][:, 0:S], T.im[:], JV(t), False, False, ["im", "jv%d" % (t % 2)], S)] if t else []
        mms(dead + [(PB[1][:, 0:S], T.kv[0:1, :], T.onesb[0:1, :], not t, False, ["kv", "onesb"], S), (PB[1][:, 0:S], IB, T.hi[:], False, False, ["shw", "hi"], S),
                    (PB[1][:, 0:S], IB, T.lw[:], False, True, ["shw", "lw"], S)], "p1")
        for a, b in ([] if t else PARTS0[1:]):
            listed(t, a, b)

    def test(t):
        jv, jk = JV(t), "jv%d" % (t % 2)
        total = 17 + (t > 1)
        done = [0]

        def flags():
            done[0] += 1
            return done[0] == 1, done[0] == total

        def count(l, r, reads):
            mms([(PB[2][:, 0:S], l, r, None, None, reads, S)], "p2", flags)

        if t > 1:
            tt(T.mis[:], T.ref[:, 0:S].indirect(T.cdl[:, 0:28]), T.nth[:], A.not_equal, ["ref", "nth", "cdl"], ["mis"], per=GAT)
            mms([(PB[4][:, 0:S], IB, T.cb[:], True, False, ["shw", "cb"], S), (PB[4][:, 0:S], T.b512[:], T.mis[:], False, True, ["b512", "mis"], S)], "p4")
            tt(jv, PB[4][:, 0:S], T.nc[:], A.min, ["p4", "nc"], [jk])
        o = S * (t % 2)
        if t < RO:
            for j in range(9):
                a = j % 8
                dma("Y", "dj%d" % (t - 1), T.jt[0:128 - 16 * a:16, S * j:S * j + S], T.jv[16 * a:128:16, o:o + S], [jk], ["jt%d" % j], 1.3)
                if a:
                    dma("Y", "dj%d" % (t - 1), T.jt[128 - 16 * a:128:16, S * j:S * j + S], T.jv[0:16 * a:16, o:o + S], [jk], ["jt%d" % j], 1.3)
        dead = [(PB[6][:, 0:S], T.ne[:], JV(t - 1), True, False, ["ne", "jv%d" % ((t - 1) % 2)], S), (PB[6][:, 0:S], T.nf[:], T.ncb[:], False, False, ["nf", "ncb"], S)] if t > 1 else []
        mms(dead + [(PB[6][:, 0:S], T.na[:], T.ncb[:], t == 1, False, ["na", "ncb"], S), (PB[6][:, 0:S], T.nb[:], T.sl[:], False, False, ["nb", "sl"], S),
                    (PB[6][:, 0:S], T.nd[:], T.ref[:], False, True, ["nd", "ref"], S)], "p6")
        ts(T.neg[:], PB[6][:, 0:S], col(13), None, A.is_gt, None, ["p6", "pf13"], ["neg"])
        count(T.i16[:], T.neg[:], ["i16", "neg"])
        if t > 1:
            count(T.i32[:], T.far[:, S - o:2 * S - o], ["i32", "far%d" % ((t - 1) % 2)])
        mms([(PB[5][:, 0:S], T.ip[:], jv, True, False, ["ip", jk], S), (PB[5][:, 0:S], T.im[:], T.ncb[:], False, False, ["im", "ncb"], S),
             (PB[5][:, 0:S], IB, SZ, False, False, ["shw", "szb"], S)], "p5")
        if t == RO:
            mms([(PB[3][:, 0:S], IB, T.ref[:], True, False, ["shw", "ref"], S), (PB[3][:, 0:S], T.i448[:], T.sl[:], False, True, ["i448", "sl"], S)], "p3")
            lin(T.yrf[:], PB[3][:, 0:S], 1.0, col(17), ["p3", "pf17"], ["yrf"])
            lin(T.yjf[:], jv, 1.0, col(18), [jk, "pf18"], ["yjf"])
            dma("Y", "ds3", T.s3[:, 0:112, :], T.yrf[:], ["yrf"], ["s3"])
            dma("Y", "ds3", T.s3[:, 112:119, :], T.yjf[0:128:16, :], ["yjf"], ["s3"])
            dma("Y", "ds3", T.r3[me, 0:112, :], T.yrf[mine, :], ["yrf"], ["r3"])
            dma("Y", "ds3", T.r3[me, 112:119, :], T.yjf[16 * me:16 * me + 1, :], ["yjf"], ["r3"])
            bulk_send(3)
        for k in range(16):
            c = slice(S * k, S * k + S)
            aim = T.tab[:, 0:9 * S].indirect(T.lt[:, 28 * k:28 * k + 28])
            if k < NA:
                tt(T.ind[:, c], aim, T.gg[:, c], A.is_lt, TAB + ["lt%d" % k, "gg%d" % k], ["ind%d" % k], per=GAT)
            else:
                act(T.gg[:, c], aim, F.Abs, TAB + ["lt%d" % k, "bk"], ["gg%d" % k], per=GAT, bias=T.bk[:, k:k + 1])
                tt(T.ind[:, c], T.gg[:, c], PB[1][:, 0:S], A.is_gt, ["gg%d" % k, "p1"], ["ind%d" % k])
            count(T.uw[:, 15 - k:143 - k], T.ind[:, c], ["uw", "ind%d" % k])
        far = T.far[:, o:o + S]
        ts(far, PB[2][:, 0:S], col(14), 0.0, A.max, A.not_equal, ["p2", "pf14"], ["far%d" % (t % 2)])
        mms([(PB[5][:, 0:S], T.b20[:], far, False, True, ["b20", "far%d" % (t % 2)], S)], "p5")
        act(T.ln[:, 8:8 + S], PB[5][:, 0:S], F.Relu, ["p5"], ["ln", "tot%d" % t], S + 170, accum_out=T.tot[:, t:t + 1])

    for t in range(RO):
        table(t)
        test(t + 1)
        if t + 1 < RO:
            sums_send(t + 1, T.mw, "mw")

    o = 64 * RO
    dma("Y", "ds4", T.s4[:], T.far[:, 0:S], ["far0"], ["s4"])
    dma("Y", "ds4", T.r4[me], T.far[mine, 0:S], ["far0"], ["r4"])
    calls = []
    for j in range(4):
        c, out = slice(Q4 * j, Q4 * j + Q4), PB[1][0:Q4, 8 * j:8 * j + 8]
        calls += [(out, T.jv[:, c], T.d64[:], True, False, ["jv0", "d64"], 8), (out, T.ncb[:, c], T.d65[:], False, False, ["ncb", "d65"], 8),
                  (out, T.far[:, c], T.d20[:], False, True, ["far0", "d20"], 8)]
    mms(calls, "p1")
    for j in range(4):
        ts(T.xs[0:Q4, o + j:o + 64:8], PB[1][0:Q4, 8 * j:8 * j + 8], 0.0, None, A.max, None, ["p1", "xz"], ["xc%d" % j], 16)
    act(T.xs[:, o + 4:o + 64:8], T.ones[:, 0:8], F.Identity, ["ones", "xz", "tot%d" % RO], ["xc4"], 16, scale=T.tot[:, RO:RO + 1])
    XC = keys("xc", 0, 5)
    small_send(RO, XC)
    bulk_send(4)
    cp(T.xr[:, o + 8 * me:o + 8 * me + 8], T.xs[:, o + 56:o + 64], XC, ["xo4"], 16)
    dma("Y", "do3", T.jrow[0:8, :], T.r3[:, 112:119, :], ["r3"], ["jrow"])
    dma("Y", "dy", T.yr[:], T.r3[:, 0:112, :], ["r3"], ["yr"])
    dma("Y", "dy", T.yj[:], T.r3[:, 112:119, :], ["r3"], ["yj"])
    ts(PB[3][0:8, 0:S], T.jrow[0:8, :], float(-S * me), None, A.add, None, ["jrow"], ["p3"])
    tt(T.al8[0:8, :], PB[3][0:8, 0:S], T.ion[0:8, :], A.is_equal, ["p3", "ion"], ["al8"])
    mms([(PB[6][:, 0:S], IB, T.szob[:], True, False, ["shw", "szob"], S), (PB[6][:, 0:S], T.rep[0:8, :], T.al8[0:8, :], False, True, ["rep", "al8"], S)], "p6")
    act(T.szal[:], PB[6][:, 0:S], F.Relu, ["p6"], ["szal"], bias=-1024.0)
    mms([(PB[4][:, 0:S], IB, T.szal[:], True, False, ["shw", "szal"], S)], "p4")
    XR = ["xr4", "xo4"]
    mms([(PB[7][:, 0:8], T.ema[:], T.xr[:, o + 4:o + 64:8], True, True, ["ema"] + XR, 256),
         (PB[7][:, 8:16], T.emb[:], T.xr[:, o + 4:o + 64:8], True, True, ["emb"] + XR, 256)], "p7")
    for h in range(2):
        lin(T.xe[:, 256 * h:256 * h + 256], T.xr[:, o:o + 64].indirect(T.xl[:, 16 * h:16 * h + 16]), 1.0, 0.0, XR + ["xl"], ["xe%d" % h], 256, GAT, "SV"[h])
    tt(T.t16[:], PB[7][:, 0:16], T.mk[:], A.mult, ["p7", "mk", "mk0"], ["t16"], 16)
    op("V", lambda: V.tensor_reduce(T.yaf[:, 0:1], T.t16[:], AX.X, A.add), ["t16"], ["yaf0"], 16)
    mms([(PB[4][:, Q4 * j:Q4 * j + Q4], T.xe[0:Q4, 128 * j:128 * j + 128], T.shw[0:Q4, 128:128 + Q4], False, j == 3, ["shw", "xe%d" % (j // 2)], Q4) for j in range(4)], "p4")
    op("V", lambda: V.tensor_tensor_scan(T.yaf[:, 1:S], T.ones[:, 0:S - 1], PB[4][:, 0:S - 1], T.yaf[:, 0:1], A.mult, A.add), ["ones", "p4", "yaf0"], ["yaf"])
    dma("Y", "dz", T.ya[:], T.yaf[:], ["yaf", "yaf0"], ["ya"])
    dma("G", "dg", T.yf[:], T.r4[:], ["r4"], ["yf"])
    issue()
    for s in cnt:
        need("G", (s, None))
